import numpy as np, ml_dtypes
CORES = [35,38,43,46]
N = 4
import mx_ref
BF = ml_dtypes.bfloat16
def gentries(a):
    return np.ascontiguousarray(a.reshape(8, 16, -1).transpose(0, 2, 1)).reshape(8, -1)
def gtable(e):
    e = np.asarray(e); return np.ascontiguousarray(e.reshape(8, -1, 16).transpose(0, 2, 1)).reshape(128, -1).astype(np.int32)
def gcols(t, e):
    v = np.concatenate([t.reshape(8, 16, -1, 4), np.zeros((8, 16, 1, 4), BF)], axis=2)
    return np.ascontiguousarray(np.stack([v[g][:, e[g]] for g in range(8)])).reshape(128, -1)
def tile(rs):
    return np.stack(rs, axis=2).reshape(128, -1).astype(BF)
def cut(t, i, w=512):
    return t[:, w * i:w * i + w]
def pick(q, e):
    c = np.concatenate([q[0].reshape(128, -1, 4), np.zeros((128, 1, 4), np.uint8)], axis=1); s = np.concatenate([q[1], np.ones((16, 1), np.uint8)], axis=1)
    return (np.ascontiguousarray(c[:, e].reshape(128, -1)), np.ascontiguousarray(s[:, e]))
def join(*qs):
    return (np.concatenate([q[0] for q in qs], axis=1), np.concatenate([q[1] for q in qs], axis=1))
def put(q, e, v):
    c, s = q[0].reshape(128, -1, 4).copy(), q[1].copy(); c[:, e] = v[0].reshape(128, -1, 4); s[:, e] = v[1]
    return (c.reshape(128, -1), s)
def pk(c, s):
    return (np.ascontiguousarray(c), mx_ref.live(s))
def emit(q):
    return q[0], q[1]
def packed(v, rng):
    q = [mx_ref.quantize(np.ascontiguousarray(v[r])) for r in range(N)]
    return np.stack([a for a, b in q]), np.stack([mx_ref.plane(b, rng) for a, b in q])
def values_of_codes():
    e, c = np.zeros((128, 128, 4), np.float32), np.zeros((128, 2, 4), np.uint8)
    e[np.arange(128), np.arange(128), 0] = 1
    c[:127, :, 0] = np.arange(256).reshape(2, 128).T[:127]
    return mx_ref.matmul(mx_ref.quantize(e.reshape(128, 512).astype(BF)), (c.reshape(128, 8), np.full((16, 2), 127, np.uint8))).T.reshape(-1).astype(np.float64)
CODE_VALUE, SCALE_VALUE = values_of_codes(), 2.0 ** (np.arange(256) - 127.0)
def decode(q):
    return (CODE_VALUE[q[0]].reshape(16, 8, -1, 4) * SCALE_VALUE[q[1]][:, None, :, None] + 0.0).reshape(128, -1).astype(np.float32)
def f(rng, *shape):
    return mx_ref.flush((rng.standard_normal(shape, dtype=np.float32) * np.exp2(rng.integers(-2, 3, shape[:-1] + (1,)))).astype(BF))
def wide(rng, *shape, cols=0):
    v = rng.standard_normal(shape, dtype=np.float32) * np.exp2(rng.integers(-12, 13, shape)).astype(np.float32)
    if cols: v *= np.repeat(np.exp2(rng.integers(-cols, cols + 1, shape[:-2] + (1, shape[-1] // 4))) * (rng.random(shape[:-2] + (1, shape[-1] // 4)) > 0.0625), 4, axis=-1).astype(np.float32)
    return mx_ref.flush(v.astype(BF))
C, T, S, R = 320, 16, 10, 3
STEP = [1, 2, 1]
def spines(root, right):
    n = np.concatenate([right, np.full((8, 1), C)], axis=1)
    s = [root]
    for i in range(S - 1): s.append(np.take_along_axis(n, s[-1], axis=1))
    return np.stack(s, axis=2).reshape(8, T * S)
def gput(t, e, h):
    a, b = np.concatenate([t.reshape(8, 16, -1, 4), np.zeros((8, 16, 1, 4), BF)], axis=2), h.reshape(8, 16, -1, 4)
    for g in range(8): a[g][:, e[g]] = b[g]
    return np.ascontiguousarray(a[:, :, :C]).reshape(128, -1)
def big(v):
    v = v.astype(np.float32)
    v[np.abs(v) < np.float32(2.0 ** -16)] = 0
    return v.astype(BF)
def numbers_of(rng):
    return {"x": big(f(rng, N, 128, 4 * C)), "u": np.array(f(rng, N, 128, 512)), "v": np.array(f(rng, N, 128, 512))}
def layers(rng):
    return big(f(rng, N, 128, 2048)).reshape(N, 8, 16, 4, 8, 16, 4)
def weights(rng, w):
    c, p = packed(np.ascontiguousarray(w).reshape(N, 128, 2048), rng)
    return {"wc": c, "ws": p}
def signs(rng):
    return rng.permutation(8) % 2 * 2.0 - 1.0
def shape(rng, own, chance, plan=()):
    left, right, n = [C] * C, [C] * C, T
    def hang(h, side, k):
        nonlocal n
        for _ in range(k):
            side[h] = n
            h, side, n = n, right, n + 1
    for m, (a, b, c) in enumerate(plan):
        hang(m, right, a - 1)
        if a > S: hang(n - 1, left, 1)
        hang(m, left, b - 1)
        hang(right[m], left, c - 2)
    way, tree = (rng.random((C, 16)) < chance[own][:, None]).tolist(), own.tolist()
    for j in range(n, C):
        h, i, side = tree[j], 0, (left, right)[way[j][0]]
        while side[h] < C:
            h, i = side[h], i + 1
            side = (left, right)[way[j][i % 16]]
        side[h] = j
    return left, right
def grown(rng):
    return shape(rng, rng.integers(0, T, C), rng.choice([0.3, 0.6, 0.8, 0.95], T))
def places(rng):
    return np.argsort(rng.random((N, 8, C)), axis=2)
def links(e, a):
    t = np.zeros((2, N, 8, C), np.int64)
    for r in range(N):
        for g in range(8):
            p = np.append(e[r, g], C)
            for i in range(2): t[i, r, g, e[r, g]] = p[a[r][g][i]]
    return {"ro": np.stack([gtable(e[r, :, :T]) for r in range(N)]), "le": np.stack([gtable(q) for q in t[0]]), "ri": np.stack([gtable(q) for q in t[1]])}
def forests(rng):
    return links(places(rng), [[grown(rng) for g in range(8)] for r in range(N)])
def setup_inputs(rng):
    return {**numbers_of(rng), **weights(rng, layers(rng)), **forests(rng)}
def setup_inputs_ties(rng):
    d = numbers_of(rng)
    e = rng.permutation(N)
    x = d["x"].reshape(N, 8, 16, C, 4)
    a = x[0][:, :8, :3].copy()
    a[:, :, 2] = 0
    for r in range(N):
        k = np.zeros(C, int) if r == e[0] else rng.permutation(C) % 3
        x[r][:, :8] = a[:, :, k]
    x[e[1]][:, :8] = 0
    u = d["u"].reshape(N, 8, 16, 8, 16, 4)
    k = u[0].copy()
    u[:, :, :, :, 0] = 0
    for g in range(8): u[:, g, :8, g, 0] = k[g, :8, g, 0]
    w = layers(rng)
    w[:, :, :, :, :, :8] = 0
    return {"x": x.reshape(N, 128, 4 * C), "u": u.reshape(N, 128, 512), "v": d["v"], **weights(rng, w), **forests(rng)}
def setup_inputs_near(rng):
    d = numbers_of(rng)
    k = forests(rng)
    x = np.zeros((N, 8, 16, C, 4), np.float32)
    u = d["u"].reshape(N, 128, 128, 4)
    u[:, :, ::16] = 0
    c, half = signs(rng), int(rng.integers(2))
    for r in range(N):
        low, up = 2 * r // N == half, int((r & STEP[0]) > 0)
        root = gentries(k["ro"][r])
        i = rng.integers(0, S, (8, C + 1))
        np.put_along_axis(i, spines(root, gentries(k["ri"][r])), np.arange(T * S)[None] % S, axis=1)
        s = (i[:, :C] + 1 + (0 if low else S * up)) // 2
        size = 2.0 ** -6 if low else 1.0
        x[r, :, 0, :, 0] = ((8 * c + up) * 2.0 ** -30 if low else c)[:, None]
        x[r, :, 8] = ((s[:, :, None] >> np.arange(4)) & 1) * np.exp2(np.arange(4) - 23.0) * size
        x[r, :, 10:] = rng.integers(4, 8, (8, 6, C, 4)) * 2.0 ** -20 * size
        if not low:
            for g in rng.permutation(8)[:4]: x[r, g, 0, root[g, rng.integers(T)], 0] *= np.float32(2.0 ** 30)
        for h in range(0, 128, 16):
            u[r, h, h, 0] = 2.0 ** -30 if low else 1.0
            u[r, h + 8, h] = 2.0 ** -30 if low else 1.0
    w = layers(rng)
    w[:, :, :10] = 0
    w[:, :, :, :, :, :10] = 0
    return {"x": x.reshape(N, 128, 4 * C).astype(BF), "u": u.reshape(N, 128, 512), "v": d["v"], **weights(rng, w), **k}
def setup_inputs_huge(rng):
    d = numbers_of(rng)
    e, a = places(rng), [grown(rng) for r in range(N)]
    x = 0.6 + 0.2 * rng.random((N, 8, 16, C, 4))
    half = int(rng.integers(2))
    for r in range(N):
        c = rng.permutation(C) % 2 if 2 * r // N != half else np.zeros(C, int)
        for g in range(8): x[r, g][:, e[r, g]] *= np.where(c > 0, 2.0 ** 29, -2.0 ** 30)[None, :, None]
    u = d["u"].reshape(N, 128, 128, 4)
    k = 2.0 ** 30 * (1 - 0.25 * rng.random((N, 128, 8, 4))) * signs(rng)[None, None, :, None]
    u[:, :, ::16] = k.astype(np.float32).astype(BF)
    w = np.zeros((N, 128, 4, 128, 4), np.float32)
    i = np.arange(128)
    for b in range(4): w[:, i, b, i, b] = 4
    return {"x": x.astype(np.float32).reshape(N, 128, 4 * C).astype(BF), "u": u.reshape(N, 128, 512), "v": d["v"], **weights(rng, w.astype(BF)), **links(e, [[a[r]] * 8 for r in range(N)])}
def setup_inputs_slots(rng):
    n = [(S + 1,) * 3] * 2 + [(S,) * 3] * 2 + [(S - 1,) * 3] + [(1, 1, 1)] * 3 + [(1, S, 1), (S, 1, 2)]
    h = rng.permutation(8)
    a = []
    for r in range(N):
        odd = bin(r).count("1") % 2
        a.append([])
        for g in range(8):
            o = rng.permutation(10)
            if g == h[0]: o = np.arange(10)
            if g == h[1]: o = (np.arange(10) + 5 * odd) % 10
            a[r].append(shape(rng, rng.integers(10, T, C), rng.choice([0.3, 0.6, 0.8, 0.95], T), [n[i] for i in o]))
    return {**numbers_of(rng), **weights(rng, layers(rng)), **links(places(rng), a)}
def setup_inputs_spread(rng):
    d = setup_inputs(rng)
    d["x"] = big(wide(rng, N, 128, 4 * C, cols=6))
    return d
def check_inputs(d):
    b = []
    for k in ("x", "u", "v"):
        a = np.abs(d[k].astype(np.float32))
        if not (np.isfinite(a).all() and ((a == 0) | (a >= 2.0 ** -30) & (a <= 2.0 ** 30)).all()): b.append("a value of " + k)
    none, least, most = [emit(mx_ref.quantize(np.full((128, 16), k, np.float32).astype(BF)))[1][0, 0] for k in (0.0, 2.0 ** -30, 2.0 ** 30)]
    for r in range(N):
        if ((d["wc"][r] == 0x7F) | (d["wc"][r] == 0xFF)).any(): b.append("wc: a code that is no number")
        s = mx_ref.live(d["ws"][r])
        if ((s != none) & ((s < least) | (s > most))).any(): b.append("ws: a scale out of range")
        root, left, right = [gentries(d[k][r]) for k in ("ro", "le", "ri")]
        if (root < 0).any() or (root >= C).any() or (left < 0).any() or (left > C).any() or (right < 0).any() or (right > C).any():
            b.append("an entry of ro, le or ri out of range")
            continue
        for g in range(8):
            k = np.bincount(np.concatenate([root[g], left[g], right[g]]), minlength=C + 1)
            if (k[:C] != 1).any(): b.append("a place that isn't once a root or a child")
            up = np.arange(C + 1)
            up[left[g]] = np.arange(C)
            up[right[g]] = np.arange(C)
            up[root[g]] = root[g]
            up[C] = C
            for i in range(10): up = up[up]
            if not np.isin(up[:C], root[g]).all(): b.append("a place that no root reaches")
    return b
def reference(x, u, v, wc, ws, ro, le, ri):
    qu = [mx_ref.quantize(u[r]) for r in range(N)]
    lay = [pk(wc[r], ws[r]) for r in range(N)]
    now = [x[r] for r in range(N)]
    root, left, right = [[gentries(a[r]) for r in range(N)] for a in (ro, le, ri)]
    for t in range(R):
        s, sent, score = [], [], []
        for r in range(N):
            s.append(spines(root[r], right[r]))
            sent.append(mx_ref.quantize(gcols(now[r], s[r])))
            score.append(mx_ref.matmul(qu[r], sent[r])[::16].reshape(8, T, S))
        came = decode(join(*sent)).astype(BF)
        for r in range(N):
            lo, hi = min(r, r ^ STEP[t]), max(r, r ^ STEP[t])
            full = [(s[i] < C).reshape(8, T, S) for i in (lo, hi)]
            key = np.concatenate([score[lo], score[hi]], axis=2) + np.float32(0.0)
            o = np.lexsort((-key, ~np.concatenate(full, axis=2)), axis=2)
            first = np.sum(full[0], axis=2, keepdims=True) * int(r == hi)
            a = np.take_along_axis(o, first + np.arange(S), axis=2)
            a = a // S * (T * S) + S * np.arange(T)[:, None] + a % S
            a = np.where(full[int(r == hi)], a, -1)
            n = np.concatenate([a[:, :, 1:], np.full((8, T, 1), -1)], axis=2)
            n = np.where(n < 0, a, n)
            both = np.concatenate([cut(came, lo, 4 * T * S), cut(came, hi, 4 * T * S)], axis=1)
            e = gcols(both, a.reshape(8, -1)).astype(np.float32)
            z = ((e + gcols(both, n.reshape(8, -1)).astype(np.float32)) * np.float32(0.5)).astype(BF)
            q = mx_ref.quantize(z)
            h = tile([np.maximum(mx_ref.matmul(pick(lay[r], np.arange(128 * b, 128 * b + 128)), q), np.float32(0.0)) * np.float32(0.03125) + e[:, b::4] for b in range(4)])
            now[r] = gput(now[r], s[r], h)
            m = np.zeros((8, C + 1), bool)
            np.put_along_axis(m, s[r], True, axis=1)
            m = m[:, :C]
            left[r], right[r] = np.where(m, right[r], left[r]), np.where(m, left[r], right[r])
    y, ol = np.zeros((N, 128, C), np.float32), np.zeros((N, 8, 2 * C), np.float32)
    oc, osc = np.zeros((N, 128, 4 * C), np.uint8), np.zeros((N, 16, C), np.uint8)
    for r in range(N):
        q = mx_ref.quantize(now[r])
        y[r] = mx_ref.matmul(mx_ref.quantize(v[r]), q)
        ol[r] = np.concatenate([left[r], right[r]], axis=1)
        oc[r], osc[r] = emit(q)
    return {"y": y, "ol": ol, "oc": oc, "osc": osc}

@@ -1,0 +1,754 @@
+from concourse.bass import DstId, RemoteDMATransfer
+from concourse.mybir import dt, AluOpType, AxisListType, ActivationFunctionType
+
+A = AluOpType
+AF = ActivationFunctionType
+C, TR, SL = 320, 16, 10
+STEP = [1, 2, 1]
+F, B, I, U, Q, P = "float32", "bfloat16", "int32", "uint16", "float8_e4m3fn_x4", "uint8"
+DWS = 1120
+XH1, XH0, XX, XH2 = 0, 640, 1280, 2624
+UNIT = 1.0 / 2048
+BIG = 1e27
+OPT = {"seed": 2, "iters": 20000, "mean": 0.2, "heat": 0.15, "cut": 7, "z": "dv", "last": "ssssvsvv", "e2": "vsss",
+       "xat": 1, "eat": 0, "near": 0.07, "far": 0.1}
+
+SCRATCH = {
+    "xt": ("sbuf", [128, 1344], B), "ut": ("sbuf", [128, 512], B), "vt": ("sbuf", [128, 512], B),
+    "wq": ("sbuf", [128, 512], Q), "wp": ("sbuf", [128, 512], P),
+    "uq": ("sbuf", [128, 128], Q), "up": ("sbuf", [128, 128], P),
+    "u2q": ("sbuf", [128, 128], Q), "u2p": ("sbuf", [128, 128], P),
+    "vq": ("sbuf", [128, 128], Q), "vp": ("sbuf", [128, 128], P),
+    "xq": ("sbuf", [128, 336], Q), "xp": ("sbuf", [128, 336], P),
+    "pxq": ("sbuf", [128, 320], Q), "pxp": ("sbuf", [128, 320], P),
+    "half": ("sbuf", [128, 516], B), "ec": ("sbuf", [128, 516], B),
+    "eq": ("sbuf", [128, 512], Q), "ep": ("sbuf", [128, 512], P),
+    "xw": ("sbuf", [128, 3264], F), "dw": ("sbuf", [128, 4 * DWS], B),
+    "b0": ("sbuf", [128, 640], B), "b0q": ("sbuf", [128, 160], Q), "b0p": ("sbuf", [128, 160], P),
+    "be": ("sbuf", [128, 1088], B), "beq": ("sbuf", [128, 272], Q), "bep": ("sbuf", [128, 272], P),
+    "pbq": ("sbuf", [128, 144], Q), "pbp": ("sbuf", [128, 144], P),
+    "lt": ("sbuf", [128, 512], B),
+    "l1q": ("sbuf", [128, 144], Q), "l1p": ("sbuf", [128, 192], P),
+    "l2q": ("sbuf", [128, 160], Q), "l2p": ("sbuf", [128, 256], P),
+    "zf": ("sbuf", [128, 512], B), "zfq": ("sbuf", [128, 256], Q), "zfp": ("sbuf", [128, 256], P),
+    "ef": ("sbuf", [128, 320], B), "tf": ("sbuf", [128, 128], F),
+    "eh": ("sbuf", [128, 1920], B), "zt": ("sbuf", [128, 1920], B),
+    "zq": ("sbuf", [128, 480], Q), "zp": ("sbuf", [128, 480], P),
+    "t2": ("sbuf", [128, 640], F),
+    "xo": ("sbuf", [128, 1280], B), "oq": ("sbuf", [128, 320], Q), "op": ("sbuf", [128, 320], P),
+    "ys": ("sbuf", [128, 320], F),
+    "ps": ("psum", [128, 4096], F),
+    "lraw": ("sbuf", [128, 44], I), "li": ("sbuf", [128, 256], I), "sm": ("sbuf", [128, 1024], F),
+    "of": ("sbuf", [128, 512], U), "uo": ("sbuf", [128, 8], U),
+    "tin": ("sbuf", [128, 704], F), "win": ("sbuf", [128, 1408], F),
+    "gg": ("sbuf", [128, 896], F), "tt": ("sbuf", [128, 896], F),
+    "io16": ("sbuf", [128, 160], B), "m16": ("sbuf", [128, 160], B), "k16": ("sbuf", [128, 160], B),
+    "sc1": ("sbuf", [128, 480], F), "sc2": ("sbuf", [128, 480], F),
+    "ones": ("sbuf", [128, 252], B), "sig": ("sbuf", [128, 402], B),
+    "thr": ("sbuf", [128, 756], F), "k21": ("sbuf", [128, 252], B),
+    "ko": ("sbuf", [128, 48], F), "snd": ("sbuf", [128, 60], F),
+    "msg0": ("sbuf", [128, 32], F), "msg1": ("sbuf", [128, 32], F), "msg2": ("sbuf", [128, 32], F),
+    "yy": ("sbuf", [128, 1008], F), "cc": ("sbuf", [128, 1296], B), "cs": ("sbuf", [128, 1200], B),
+    "cw": ("sbuf", [128, 96], F), "mm": ("sbuf", [128, 848], F), "ms": ("sbuf", [128, 848], F),
+    "lab": ("sbuf", [128, 432], F), "ws_": ("sbuf", [128, 1104], F), "wt": ("sbuf", [128, 640], F),
+    "oi": ("sbuf", [128, 64], F), "ot": ("sbuf", [128, 64], F),
+}
+ENG = ["v", "s", "p", "g", "y"]
+ARR = ["ax", "axs", "ab", "abs_", "ak0", "ak1", "ak2", "al1", "al2"]
+SEMAPHORES = ["e" + k for k in ENG] + ARR + ["sent"] + ["d%d" % k for k in range(48)]
+WIDTH = {F: 4, B: 2, I: 4, U: 2, Q: 4, P: 1}
+CYC = 0.001
+GAT = 1.6
+KEPT = {}
+
+
+def R(name, a, b, s=1):
+    return (name, a, b, s)
+
+
+def size(r):
+    return len(range(r[1], r[2], r[3]))
+
+
+def bits(r):
+    if r[0] == "ps":
+        m = 0
+        for k in range(r[1] // 512, (r[2] - 1) // 512 + 1):
+            m |= 1 << k
+        return m
+    if r[3] == 1:
+        return ((1 << (r[2] - r[1])) - 1) << r[1]
+    m = 0
+    for k in range(r[1], r[2], r[3]):
+        m |= 1 << k
+    return m
+
+
+def build(g, core, T, topo, rank):
+    ops = []
+    eng = {"v": g.vector, "s": g.scalar, "p": g.tensor, "g": g, "y": g.sync}
+
+    def ap(r):
+        if not isinstance(r, tuple):
+            return r
+        return T[r[0]][:, r[1]:r[2]] if r[3] == 1 else T[r[0]][:, r[1]:r[2]:r[3]]
+
+    def ind(w, o):
+        return ap(w).indirect(ap(o))
+
+    def add(e, fn, rd, wr, cost, kind="c", lat=0.0, after=None, sem=None, cnt=0):
+        ops.append({"e": e, "fn": fn, "rd": [r for r in rd if isinstance(r, tuple)], "wr": wr, "cost": cost,
+                    "kind": kind, "lat": lat, "after": after, "sem": sem, "cnt": cnt})
+        return len(ops) - 1
+
+    def narrow(*rs):
+        return all(WIDTH[SCRATCH[r[0]][2]] == 2 for r in rs)
+
+    def cost(n, o=None, f=1.0):
+        return CYC * (60 + GAT * n if o else max(64, n * f))
+
+    def src(r, o):
+        return ind(r, o) if o else ap(r)
+
+    def ts(out, in0, s1, s2, op0, op1=None, o=None):
+        def fn():
+            if op1 is None:
+                return g.vector.tensor_scalar(ap(out), src(in0, o), ap(s1), None, op0)
+            return g.vector.tensor_scalar(ap(out), src(in0, o), ap(s1), ap(s2), op0, op1)
+        add("v", fn, [in0, s1, s2, o], [out], cost(size(out), o, 0.5 if narrow(out, in0) else 1.0))
+
+    def tt(out, in0, in1, op, o=None):
+        f = 1.0 if "ps" in (in0[0], in1[0]) else 2.0
+        add("v", lambda: g.vector.tensor_tensor(ap(out), src(in0, o), ap(in1), op), [in0, in1, o], [out], cost(size(out), o, f))
+
+    def cp(out, in_, o=None):
+        add("v", lambda: g.vector.tensor_copy(ap(out), src(in_, o)), [in_, o], [out], cost(size(out), o, 0.5 if narrow(out, in_) else 1.0))
+
+    def act(out, in_, func=AF.Copy, scale=1.0, bias=None, o=None):
+        def fn():
+            if bias is not None:
+                return g.scalar.activation(ap(out), src(in_, o), func, bias=ap(bias), scale=scale)
+            if scale != 1.0:
+                return g.scalar.activation(ap(out), src(in_, o), func, scale=scale)
+            return g.scalar.activation(ap(out), src(in_, o), func)
+        add("s", fn, [in_, o, bias], [out], cost(size(out), o) + 0.02)
+
+    def lin(out, in_, scale, bias, func=AF.Identity):
+        act(out, in_, func, float(scale), bias if isinstance(bias, tuple) else float(bias))
+
+    def gat(e, out, w, o, scale=1.0):
+        if e == "s":
+            act(out, w, AF.Copy, scale, None, o)
+        elif scale == 1.0:
+            cp(out, w, o)
+        else:
+            ts(out, w, scale, None, A.mult, None, o)
+
+    def scan(out, d0, d1, op0, op1, init=0.0):
+        add("v", lambda: g.vector.tensor_tensor_scan(ap(out), ap(d0), ap(d1), init, op0, op1), [d0, d1], [out],
+            cost(size(out), None, 0.5 if narrow(out, d0, d1) else 1.0))
+
+    def red(out, in_):
+        add("v", lambda: g.vector.tensor_reduce(ap(out), ap(in_), AxisListType.X, A.add), [in_], [out], cost(size(in_)))
+
+    def tr(out, in_):
+        add("v", lambda: g.vector.transpose(ap(out), ap(in_)), [in_], [out], cost(size(out)))
+
+    def mset(out, val):
+        add("v", lambda: g.vector.memset(ap(out), val), [], [out], cost(size(out), None, 0.5 if narrow(out) else 1.0))
+
+    def iota(out, pat, base, ch):
+        def fn():
+            if SCRATCH[out[0]][2] == I:
+                return g.iota(ap(out), pat, base, ch)
+            return g.iota(ap(out), pat, base, ch, allow_small_or_imprecise_dtypes=True)
+        add("g", fn, [], [out], 0.14 + 2 * CYC * size(out))
+
+    def asel(out, in_, pat, op, fill, base, ch):
+        add("g", lambda: g.affine_select(ap(out), ap(in_), pat, op, fill, base, ch), [in_], [out], 0.18 + 2 * CYC * size(out))
+
+    def quant(q, p, a, b, in_):
+        add("v", lambda: g.vector.quantize_mx(ap(R(q, a, b)), ap(R(p, a, b)), ap(in_)), [in_], [R(q, a, b), R(p, a, b)],
+            0.02 + 0.00025 * size(in_))
+
+    def mm(bank, wq, wp, wa, xq, xp, a, b):
+        out = R("ps", 512 * bank, 512 * bank + b - a)
+        rs = [R(wq, wa, wa + 128), R(wp, wa, wa + 128), R(xq, a, b), R(xp, a, b)]
+        add("p", lambda: g.tensor.matmul_mx(ap(out), ap(rs[0]), ap(rs[1]), ap(rs[2]), ap(rs[3]), True, True), rs, [out],
+            0.0008 * (b - a + 16))
+
+    def dma(e, out, in_, rd, wr, lat, acc=False):
+        def fn():
+            if acc:
+                return g.dma_start(out(), in_(), accum_op=A.add)
+            return eng[e].dma_start(out(), in_())
+        add(e, fn, rd, wr, 0.9 if e == "g" else 0.08, "d", lat)
+
+    def accumulate(out, in_):
+        dma("g", lambda: ap(out), lambda: ap(in_), [in_, out], [out], 2.5, True)
+
+    def u8(r):
+        return ap(r).bitcast(dt.uint8) if SCRATCH[r[0]][2] == Q else ap(r)
+
+    def mask(es):
+        return sum(1 << e for e in es)
+
+    def send(peer, pairs, sem, part, lat):
+        rid, pid = topo.addr(peer)[:2]
+        es = part(topo.engines(core, peer))
+        def fn():
+            if len(pairs) == 1:
+                return g.remote_dma(u8(pairs[0][1]), u8(pairs[0][0]), T.sem[sem], T.sem.sent, pid, rid, mask(es[0]))
+            return g.remote_dma_fused([RemoteDMATransfer(dst_ids=[DstId(rid=rid, pnc=pid)], dma_engine_mask=mask(es[k]),
+                                                         remote_sem=T.sem[sem], src=u8(pairs[k][0]), dst=u8(pairs[k][1]))
+                                       for k in range(len(pairs))], local_sem=T.sem.sent)
+        n = sum(len(e) for e in es)
+        k = add("g", fn, [p[0] for p in pairs], [], 0.5, "r", cnt=n)
+        add("a", None, [], [p[1] for p in pairs], 0.0, "a", lat, k, sem, n)
+
+    free = {"sm": 0, "of": 0, "li": 0}
+
+    def new(buf, n):
+        a = free[buf]
+        free[buf] = a + n + (n & 1)
+        return R(buf, a, a + n)
+
+    def sub(r, a, b, s=1):
+        return R(r[0], r[1] + a * r[3], min(r[2], r[1] + b * r[3]), r[3] * s)
+
+    def bank(k, a, b):
+        return R("ps", 512 * k + a, 512 * k + b)
+
+    peer = [T.cores[rank ^ s] for s in STEP]
+    low = [rank < (rank ^ s) for s in STEP]
+    first = [0 if l else SL for l in low]
+    pfirst = [SL - f for f in first]
+    chip = [topo.chip(core) == topo.chip(p) for p in peer]
+    allE = lambda es: [es]
+    if_on = lambda t, on, off: on if chip[t] else off
+
+    dma("y", lambda: T.lraw[:, 0:20], lambda: T.ri[:], [], [R("lraw", 0, 20)], 1.9)
+    dma("s", lambda: T.lraw[:, 40:41], lambda: T.ro[:], [], [R("lraw", 40, 41)], 1.9)
+    dma("y", lambda: T.lraw[:, 20:40], lambda: T.le[:], [], [R("lraw", 20, 40)], 1.9)
+    dma("s", lambda: T.xt[:, 0:1280], lambda: T.x[:], [], [R("xt", 0, 1280)], 3.0)
+    dma("y", lambda: T.ut[:], lambda: T.u[:], [], [R("ut", 0, 512)], 3.3)
+    dma("y", lambda: T.wq[:].bitcast(dt.uint8), lambda: T.wc[:], [R("ut", 0, 512)], [R("wq", 0, 512)], 3.0)
+    dma("y", lambda: T.wp[:], lambda: T.ws[:], [R("ut", 0, 512)], [R("wp", 0, 512)], 3.0)
+    dma("y", lambda: T.vt[:], lambda: T.v[:], [R("ut", 0, 512)], [R("vt", 0, 512)], 3.0)
+
+    pi, pj = new("li", 2), new("li", 2)
+    iota(pi, [[16, 2]], 0, 1)
+    mcol, h16, nh16 = new("sm", 1), new("sm", 1), new("sm", 1)
+    ti = new("li", 2)
+    ts(sub(ti, 0, 1), sub(pi, 0, 1), 16, None, A.bitwise_and)
+    cp(h16, sub(ti, 0, 1))
+    ts(sub(ti, 1, 2), sub(pi, 0, 1), 15, None, A.bitwise_and)
+    cp(mcol, sub(ti, 1, 2))
+    ts(pj, pi, 31, None, A.bitwise_and)
+    oroot = new("of", 2)
+    ts(oroot, pj, 672.0, None, A.add)
+    lin(nh16, h16, -1.0, 0.0)
+    mset(R("tin", 0, 704), 0.0)
+    zz = new("sm", 2)
+    mset(zz, 0.0)
+    ts(R("tin", 640, 672, 16), zz, h16, 640.0, A.add, A.add)
+    mset(R("half", 0, 516), 0.5)
+    asel(R("ec", 0, 516), R("half", 0, 516), [[-1, 516]], A.is_equal, 0.0, 3, 4)
+    for b in range(4):
+        quant("eq", "ep", 128 * b, 128 * b + 128, R("ec", 3 - b, 515 - b))
+    iota(R("zf", 0, 512), [[0, 512]], 0, 0)
+    iota(R("lt", 0, 512), [[0, 512]], 0, 0)
+    mset(R("xt", 1280, 1344), 0.0)
+    mset(R("dw", 1104, 4 * DWS, DWS), 0.0)
+    mset(R("cw", 20, 96, 32), 0.0)
+    mset(R("ones", 0, 252), 1.0)
+    iota(R("io16", 0, 160), [[0, 10], [1, 16]], 0, 0)
+    ts(R("m16", 0, 160), R("io16", 0, 160), mcol, None, A.is_equal)
+    asel(R("k16", 0, 160), R("ones", 0, 160), [[0, 10], [1, 16]], A.is_gt, 0.0, 0, 0)
+    qi = new("li", 28)
+    iota(qi, [[16, 28]], 0, 0)
+    cp(R("uo", 0, 8), sub(qi, 0, 8))
+    q = new("sm", 28)
+    ts(q, qi, mcol, None, A.add)
+    ne, qe = new("sm", 10), new("sm", 10)
+    iota(ne, [[-2048, 10]], 0, 0)
+    tt(qe, sub(q, 0, 10), ne, A.add)
+    q7, f7, i7, t7, j7, mn, mx = new("sm", 7), new("sm", 7), new("li", 7), new("sm", 7), new("sm", 7), new("sm", 7), new("sm", 7)
+    lin(q7, sub(q, 0, 7), 1.0, -12.0, AF.Relu)
+    lin(f7, q7, 0.1, -0.45)
+    cp(i7, f7)
+    ts(t7, i7, -10.0, None, A.mult)
+    tt(j7, t7, q7, A.add)
+    tt(mn, j7, i7, A.min)
+    tt(mx, j7, i7, A.max)
+    orho, oj, omn, omx, otr = new("of", 7), new("of", 7), new("of", 7), new("of", 7), new("of", 7)
+    cp(orho, i7); cp(oj, j7); cp(omn, mn); cp(omx, mx)
+    j10, j11 = new("sm", 7), new("sm", 7)
+    lin(j10, j7, 10.0, 0.0)
+    tt(j11, j10, i7, A.add)
+    ts(otr, j11, 2.0, None, A.mult)
+    f15, i15, t15, e15 = new("sm", 15), new("li", 15), new("sm", 15), new("sm", 15)
+    lin(f15, sub(q, 0, 15), 1.0 / 21, -10.0 / 21)
+    cp(i15, f15)
+    ts(t15, i15, -21.0, None, A.mult)
+    tt(e15, t15, sub(q, 0, 15), A.add)
+    oseg = new("of", 15)
+    cp(oseg, e15)
+    for t in range(3):
+        iota(R("thr", 252 * t, 252 * t + 252), [[1, 12], [0, 21]], 0, 0)
+    mset(R("thr", 20, 756, 252), 1000.0)
+    asel(R("k21", 0, 252), R("ones", 0, 252), [[0, 12], [1, 21]], A.is_gt, 0.0, 0, 0)
+    asel(R("sig", 1, 201), R("ones", 0, 200), [[-1, 10], [1, 10], [0, 2]], A.is_ge, -1.0, 0, 0)
+    asel(R("sig", 201, 401), R("ones", 0, 200), [[1, 10], [-1, 10], [0, 2]], A.is_gt, -1.0, 0, 0)
+    mset(R("sig", 0, 400, 20), 0.0)
+
+    t41, pv = new("li", 41), new("sm", 41)
+    ts(t41, R("lraw", 0, 41), 496, None, A.bitwise_and)
+    tt(pv, t41, R("lraw", 0, 41), A.add)
+    for o in (0, 16):
+        ts(R("tin", o, 640, 32), sub(pv, 0, 20), h16, None, A.add)
+    ts(R("tin", 672, 704, 16), zz, sub(pv, 40, 41), h16, A.add, A.add)
+    tr(R("win", 0, 704), R("tin", 0, 704))
+    for o in (0, 16):
+        lin(R("tin", o, 640, 32), sub(pv, 20, 40), 1.0, h16)
+    for k in range(11):
+        tr(R("win", 704 + 64 * k, 768 + 64 * k), R("tin", 64 * k, 64 * k + 64))
+    quant("xq", "xp", 0, 160, R("xt", 0, 640))
+    quant("xq", "xp", 160, 336, R("xt", 640, 1344))
+    WR, WL = R("win", 0, 704), R("win", 704, 1408)
+    oc0, oc1 = new("of", 18), new("of", 32)
+    for i in range(SL):
+        gat("v", R("gg", 32 * i, 32 * i + 32), WR, oroot if i == 0 else sub(oc0, 2 * i - 2, 2 * i))
+        if i == OPT["xat"]:
+            ops[-1]["rd"].append(R("xp", 0, 336))
+        if i == OPT["eat"]:
+            ops[-1]["rd"].append(R("ep", 0, 512))
+        tr(R("tt", 32 * i, 32 * i + 32), R("gg", 32 * i, 32 * i + 32))
+        if i < SL - 1:
+            cp(sub(oc0, 2 * i, 2 * i + 2), R("tt", 32 * i, 32 * i + 32, 16))
+    for s in range(9):
+        a = 320 + 64 * s
+        gat("s", R("gg", a, a + 64), WL if s == 0 else WR, sub(oc0, 0, 4) if s == 0 else sub(oc1, 4 * s - 4, 4 * s))
+        tr(R("tt", a, a + 64), R("gg", a, a + 64))
+        if s < 8:
+            cp(sub(oc1, 4 * s, 4 * s + 4), R("tt", a, a + 64, 16))
+
+    def places(pos, out):
+        n = size(pos)
+        ki, t = new("li", n), new("sm", n)
+        ts(ki, pos, nh16, 1.0 / 32, A.add, A.mult)
+        ts(t, ki, -16.0, nh16, A.mult, A.add)
+        tt(out, t, pos, A.add)
+
+    CA = new("sm", 36)
+    CR = [sub(CA, 12 * t, 12 * t + 12) for t in range(3)]
+    mset(sub(CA, 10, 36, 12), float(C))
+
+    send(peer[0], [(R("xq", 0, 320), R("pxq", 0, 320))], "ax", allE, 2.5)
+    send(peer[0], [(R("xp", 0, 320), R("pxp", 0, 320))], "axs", allE, 2.5)
+    for b in range(4):
+        act(R("xw", XX + 336 * b, XX + 336 * b + 336), R("xt", b, 1344, 4), AF.Copy, 0.5)
+    quant("uq", "up", 0, 128, R("ut", 0, 512))
+    add("v", lambda: g.vector.tensor_copy(T.u2q[:, 0:128].bitcast(dt.uint32), T.uq[:, 0:128].bitcast(dt.uint32).indirect(T.uo[:, 0:8])),
+        [R("uq", 0, 128), R("uo", 0, 8)], [R("u2q", 0, 128)], cost(128, True))
+    act(R("u2p", 0, 128), R("up", 0, 128), AF.Copy, 1.0, None, R("uo", 0, 8))
+
+    def decode(qn, pn, n, at, b0):
+        for b in range(4):
+            mm(b0 or b, "eq", "ep", 128 * b, qn, pn, 0, n)
+            act(R("dw", DWS * b + at, DWS * b + at + n), bank(b0 or b, 0, n))
+
+    decode("xq", "xp", 336, 608, 0)
+
+    def xwin(b):
+        return R("xw", XX + 336 * b, XX + 336 * b + 336)
+
+    for (a, z, es) in ((0, OPT["cut"], "ssss"), (OPT["cut"], SL, "vsvs")):
+        o = new("of", z - a)
+        places(R("tt", 32 * a, 32 * z, 32), sub(CR[0], a, z))
+        cp(o, sub(CR[0], a, z))
+        for b in range(4):
+            gat(es[b], R("b0", 64 * a + b, 64 * z, 4), xwin(b), o, 2.0)
+    quant("b0q", "b0p", 0, 160, R("b0", 0, 640))
+    mm(4, "u2q", "u2p", 0, "b0q", "b0p", 0, 160)
+
+    def diag(bk, n, at):
+        tt(R("sc1", at, at + n), bank(bk, 0, n), R("m16", 0, n), A.mult)
+        scan(R("sc2", at, at + n), R("k16", 0, n), R("sc1", at, at + n), A.mult, A.add)
+        return R("sc2", at + 15, at + n, 16)
+
+    KO = [R("ko", 16 * t, 16 * t + 10) for t in range(3)]
+    SK = [R("snd", 20 * t, 20 * t + 10) for t in range(3)]
+    SB = [R("snd", 20 * t + 10, 20 * t + 20) for t in range(3)]
+    MS = ["msg0", "msg1", "msg2"]
+    cap, ncap, nl, e4, kn = [], [], [], [], []
+    ZC = [640, 928, 816]
+    WIN = [(288, 944), (0, 944), (288, 1105)]
+    OWN = [(320, 0, 0), (608, 144, 1), (320, 656, 2)]
+    PAR = [(0, 0, 0), (None, 272, 1), (0, 784, 2)]
+
+    def tables(t):
+        c = sub(CR[t], 0, 10)
+        for l in (cap, ncap, nl, e4, kn):
+            l.append(new("sm", 10))
+        lin(cap[t], c, -BIG, 319.5 * BIG)
+        lin(ncap[t], c, BIG if low[t] else -BIG, (-319.5 if low[t] else 319.5) * BIG)
+        late = OWN[t][2]
+        ce = new("sm", 10)
+        tt(ce, c, ne, A.add)
+        for (dst, k, (cx, cl, _)) in ((SB[t], 20.0 - pfirst[t], PAR[t]), (R(MS[t], 20, 30), 10.0 - first[t], OWN[t])):
+            if cx is None:
+                lin(sub(dst, late, 10), sub(qe, late, 10), UNIT, k - 16 * UNIT)
+            else:
+                lin(sub(dst, late, 10), sub(ce, late, 10), UNIT, k + cx * UNIT)
+            if late:
+                lin(sub(dst, 0, late), sub(qe, 0, late), UNIT, k + cl * UNIT)
+        lin(e4[t], c, 4.0, -4.0 * (C - 1), AF.Relu)
+        iota(kn[t], [[-1, 10]], -1 - first[t], 0)
+        lin(nl[t], sub(CR[t], 1, 11), -8.0, 8.0 * C)
+
+    def keys(t, s, a, b):
+        tt(sub(SK[t], a, b), s, sub(ncap[t], a, b), A.max if low[t] else A.min)
+        tt(sub(KO[t], a, b), s, sub(cap[t], a, b), A.min)
+
+    def send_keys(t):
+        send(peer[t], [(R("snd", 20 * t, 20 * t + 20), R(MS[t], 0, 20))], "ak%d" % t,
+             if_on(t, lambda es: [es[len(es) // 2:]], allE), 1.6)
+
+    tables(0)
+    keys(0, diag(4, 160, 0), 0, 10)
+    send_keys(0)
+    decode("pxq", "pxp", 320, 288, 0)
+
+    c12 = new("sm", 18)
+    places(R("tt", 320, 896, 32), c12)
+    ob1, ob2 = new("of", 9), new("of", 8)
+    cp(ob1, sub(c12, 0, 18, 2))
+    cp(ob2, sub(c12, 1, 17, 2))
+    act(sub(CR[1], 0, 1), sub(CR[0], 0, 1)); act(sub(CR[1], 1, 10), sub(c12, 0, 18, 2))
+    act(sub(CR[2], 0, 2), sub(CR[0], 0, 2)); act(sub(CR[2], 2, 10), sub(c12, 1, 17, 2))
+    for b in range(4):
+        gat("s", R("be", b, 576, 4), xwin(b), ob1, 2.0)
+    for b in range(4):
+        gat("s", R("be", 576 + b, 1088, 4), xwin(b), ob2, 2.0)
+    quant("beq", "bep", 0, 144, R("be", 0, 576))
+    quant("beq", "bep", 144, 272, R("be", 576, 1088))
+    send(peer[1], [(R("beq", 0, 144), R("pbq", 0, 144))], "ab", allE, 2.5)
+    send(peer[1], [(R("bep", 0, 144), R("pbp", 0, 144))], "abs_", allE, 2.5)
+    mm(5, "u2q", "u2p", 0, "beq", "bep", 0, 144)
+    tables(1); tables(2)
+    keys(1, diag(5, 144, 160), 1, 10)
+    mm(5, "u2q", "u2p", 0, "beq", "bep", 144, 272)
+    keys(2, diag(5, 128, 304), 2, 10)
+
+    def last_lists():
+        iota(R("lab", 0, 160), [[1, 160]], XH2, 0)
+        iota(R("lab", 160, 288), [[4, 128]], XH0 + 128, 0)
+        iota(R("lab", 288, 432), [[4, 144]], XH1 + 64, 0)
+        pa, pb, dm = new("sm", 27), new("sm", 27), new("sm", 27)
+        lin(dm, sub(q, 0, 27), 1.0, 672.0)
+        act(sub(pa, 0, 2), R("tt", 0, 64, 32))
+        act(sub(pa, 2, 10), R("tt", 352, 864, 64))
+        act(sub(pa, 10, 18), R("tt", 64, 320, 32))
+        act(sub(pa, 18, 27), R("tt", 320, 896, 64))
+        lin(pb, pa, 2000.0, -639.0 * 2000.0)
+        tt(pb, pb, dm, A.min)
+        tt(pb, pb, pa, A.max)
+        osc = new("of", 27)
+        cp(osc, pb)
+        iota(R("ws_", 0, 640), [[0, 640]], 0, 0)
+        for a in range(0, 27, 6):
+            o = sub(osc, a, min(a + 6, 27))
+            s = R("lab", 16 * a, 16 * min(a + 6, 27))
+            add("v", lambda o=o, s=s: g.vector.tensor_copy(ind(R("ws_", 0, 1104), o), ap(s)), [o, s], [R("ws_", 0, 1104)],
+                CYC * (60 + 3.5 * size(s)))
+        for k in range(4):
+            tr(R("wt", 160 * k, 160 * k + 160), R("ws_", 160 * k, 160 * k + 160))
+        lb, f0, xi, x2, ix = new("sm", 20), new("sm", 20), new("sm", 20), new("sm", 20), new("sm", 20)
+        s1, s2, st = new("sm", 20), new("sm", 20), new("sm", 20)
+        tt(lb, R("wt", 0, 640, 32), R("wt", 16, 640, 32), A.add)
+        lin(xi, sub(q, 0, 20), 1.0, float(XX))
+        lin(f0, lb, -1.0, 1.0, AF.Relu)
+        tt(x2, xi, f0, A.mult)
+        tt(ix, x2, lb, A.add)
+        lin(s1, f0, 335.0, 1.0)
+        ts(s2, lb, float(XH2), 159.0, A.is_ge, A.mult)
+        tt(st, s1, s2, A.add)
+        out = []
+        for b in range(4):
+            out.append(new("of", 20))
+            cp(out[b], ix)
+            if b < 3:
+                nx = new("sm", 20)
+                tt(nx, ix, st, A.add)
+                ix = nx
+        f1, f2, d = new("sm", 20), new("sm", 20), new("sm", 20)
+        lin(f1, lb, 1.0, -(XH2 + 23.5), AF.Abs)
+        ts(f2, f1, 8.0, None, A.is_lt)
+        tt(f2, f2, f0, A.add)
+        tt(d, R("lraw", 20, 40), R("lraw", 0, 20), A.subtract)
+        tt(d, d, f2, A.mult)
+        iota(R("oi", 0, 64), [[0, 64]], 0, 0)
+        tt(R("oi", 0, 20), d, R("lraw", 0, 20), A.add)
+        tt(R("oi", 32, 52), R("lraw", 20, 40), d, A.subtract)
+        tr(R("ot", 0, 64), R("oi", 0, 64))
+        for gr in range(8):
+            for s in range(2):
+                p0, c0 = 32 * (gr // 2), 32 * s + 16 * (gr % 2)
+                dma("y", lambda gr=gr, s=s: T.ol[gr:gr + 1, C * s:C * s + C], lambda p0=p0, c0=c0: T.ot[p0:p0 + 20, c0:c0 + 16],
+                    [R("ot", 0, 64)], [], 2.0)
+        return out
+
+    def order(t):
+        y0, c0, s0 = 336 * t, 432 * t, 400 * t
+        PK = R(MS[t], 0, 10)
+        Y = [R("yy", y0 + 112 * k, y0 + 112 * k + 112) for k in range(3)]
+        gat("s", Y[0], KO[t], omx)
+        gat("s", Y[1], KO[t], orho)
+        tt(R("cc", c0 + 201, c0 + 424, 2), KO[t], Y[0], A.is_ge, omn)
+        gat("s", Y[2], PK, omx)
+        tt(R("cc", c0 + 200, c0 + 424, 2), PK, Y[1], A.is_gt if low[t] else A.is_ge, oj)
+        gat("s", R("cc", c0, c0 + 224, 2), R("cc", c0 + 224, c0 + 424), otr)
+        tt(R("cc", c0 + 1, c0 + 224, 2), PK, Y[2], A.is_ge, omn)
+        scan(R("thr", 252 * t + 41, 252 * t + 232, 21), kn[t], e4[t], A.add, A.subtract, 1000.0)
+        scan(R("cs", s0, s0 + 400), R("sig", 0, 400), R("cc", c0 + 24, c0 + 424), A.mult, A.add)
+        tt(R("cw", 32 * t, 32 * t + 20), R(MS[t], 10, 30), R("cs", s0 + 19, s0 + 400, 20), A.subtract)
+
+    DF = new("sm", 36)
+    mset(sub(DF, 10, 36, 12), 4.0)
+
+    def sources(t, at, n, k):
+        tt(R("mm", at, at + n), R("cw", 32 * t, 32 * t + 21), R("thr", 252 * t, 252 * t + n), A.max, sub(oseg, 0, n // 16))
+        scan(R("ms", at, at + n), R("k21", 0, n), R("mm", at, at + n), A.mult, A.add)
+        df = sub(DF, 12 * t, 12 * t + 11) if k == 10 else new("sm", k + 1)
+        tt(sub(df, 0, k), R("ms", at + 20, at + 21 * k, 21), R("ms", at + 41, at + 21 * k + 21, 21), A.subtract)
+        return df
+
+    def dwin(t, b):
+        return R("dw", DWS * b + WIN[t][0], DWS * b + WIN[t][1])
+
+    def fast(t):
+        df = sources(t, 720 + 64 * t, 64, 2)
+        oa, on, nf = new("of", 1), new("of", 1), new("sm", 1)
+        ts(oa, sub(df, 0, 1), 2048.0, None, A.mult)
+        ts(nf, sub(df, 0, 1), sub(nl[t], 0, 1), sub(df, 1, 2), A.add, A.min)
+        ts(on, nf, 2048.0, None, A.mult)
+        e0 = 128 * t
+        for b in range(4):
+            gat("s", R("ef", e0 + b, e0 + 64, 4), dwin(t, b), oa)
+            tt(R("zf", b, 64, 4), dwin(t, b), R("ef", e0 + b, e0 + 64, 4), A.add, on)
+        act(R("ef", e0 + 64, e0 + 128), R("ef", e0, e0 + 64), AF.Copy, 2.0)
+        quant("zfq", "zfp", 128 * t, 128 * t + 128, R("zf", 0, 512))
+        for b in range(4):
+            mm(b, "wq", "wp", 128 * b, "zfq", "zfp", 128 * t, 128 * t + 128)
+            act(R("tf", 64 * t + b, 64 * t + 64, 4), bank(b, 0, 16), AF.Relu, 0.03125)
+        tt(R("lt", 0, 64), R("tf", 64 * t, 64 * t + 64), R("ef", e0 + 64, e0 + 128), A.add)
+        qn, pn, n = ("l1q", "l1p", 16) if t == 0 else ("l2q", "l2p", 32)
+        quant(qn, pn, 0, 128, R("lt", 0, 512))
+        send(peer[t + 1], [(R(qn, 0, n), R(qn, 128, 128 + n)), (R(pn, 0, 4 * n), R(pn, 128, 128 + 4 * n))], "al%d" % (t + 1),
+             if_on(t + 1, lambda es: [es[:len(es) // 4], es[len(es) // 4:len(es) // 2]],
+                   lambda es: [es[:len(es) // 2], es[len(es) // 2:]]), 2.0)
+        mm(4, "u2q", "u2p", 0, qn, pn, 0, 128)
+        if t == 0:
+            tt(R("sc1", 432, 448), bank(4, 0, 16), R("m16", 0, 16), A.mult)
+            red(sub(SK[1], 0, 1), R("sc1", 432, 448))
+            red(sub(KO[1], 0, 1), R("sc1", 432, 448))
+        else:
+            keys(2, diag(4, 32, 448), 0, 2)
+        send_keys(t + 1)
+
+    def full(t):
+        df = sources(t, 240 * t, 240, 10)
+        oa, on, nf = new("of", 10), new("of", 10), new("sm", 10)
+        ts(oa, sub(df, 0, 10), 2048.0, float(ZC[t]), A.mult, A.min)
+        tt(nf, sub(df, 0, 10), nl[t], A.add)
+        tt(nf, nf, sub(df, 1, 11), A.min)
+        ts(on, nf, 2048.0, float(ZC[t]), A.mult, A.min)
+        e0 = 640 * t
+        E = [R("eh", e0 + b, e0 + 640, 4) if t < 2 else R("eh", e0 + 160 * b, e0 + 160 * b + 160) for b in range(4)]
+        for b in range(4):
+            gat(OPT["e2"][b] if t == 2 else "s", E[b], dwin(t, b), oa)
+            if t < 2 and OPT["z"][t] == "d":
+                gat("s", R("zt", e0 + b, e0 + 640, 4), dwin(t, b), on)
+            else:
+                tt(R("zt", e0 + b, e0 + 640, 4), dwin(t, b), E[b], A.add, on)
+        if t < 2 and OPT["z"][t] == "d":
+            accumulate(R("zt", e0, e0 + 640), R("eh", e0, e0 + 640))
+        quant("zq", "zp", 160 * t, 160 * t + 160, R("zt", e0, e0 + 640))
+        h0 = [XH0, XH1, XH2][t]
+        if t == 0:
+            e1, o1 = new("sm", 1), new("of", 1)
+            lin(e1, sub(CR[0], 1, 2), 16.0, 0.0)
+            ts(o1, e1, -16.0 * (C - 1), mcol, A.add, A.max)
+            mset(R("t2", 16, 128, 32), 0.0)
+            act(R("ef", 256, 320), R("eh", 64, 128), AF.Copy, 2.0)
+        for b in range(4):
+            bk = b if t == 2 else 6 + (b & 1)
+            mm(bk, "wq", "wp", 128 * b, "zq", "zp", 160 * t, 160 * t + 160)
+            if t == 0:
+                w = R("t2", 32 * b, 32 * b + 17)
+                act(sub(w, 0, 16), bank(bk, 16, 32), AF.Relu, 0.03125)
+                tt(R("lt", 64 + b, 128, 4), w, R("ef", 256 + b, 320, 4), A.add, o1)
+            if t < 2:
+                act(R("xw", h0 + b, h0 + 640, 4), bank(bk, 0, 160), AF.Relu, 0.015625)
+            else:
+                act(R("t2", 160 * b, 160 * b + 160), bank(b, 0, 160), AF.Relu, 0.015625)
+                tt(R("xw", h0 + 160 * b, h0 + 160 * b + 160), R("t2", 160 * b, 160 * b + 160), E[b], A.add)
+        if t < 2:
+            accumulate(R("xw", h0, h0 + 640), R("eh", e0, e0 + 640))
+
+    order(0)
+    fast(0)
+    decode("pbq", "pbp", 144, 0, 5)
+    full(0)
+    order(1)
+    decode("l1q", "l1p", 144, 144, 0)
+    fast(1)
+    full(1)
+    olast = last_lists()
+    quant("vq", "vp", 0, 128, R("vt", 0, 512))
+    order(2)
+    decode("l2q", "l2p", 160, 944, 0)
+    full(2)
+    for b in range(4):
+        for h in range(2):
+            gat(OPT["last"][2 * b + h], R("xo", 640 * h + b, 640 * h + 640, 4), R("xw", 0, XH2 + 160 * b + 160),
+                sub(olast[b], 10 * h, 10 * h + 10), 2.0)
+    for h in range(2):
+        a, z = 160 * h, 160 * h + 160
+        quant("oq", "op", a, z, R("xo", 4 * a, 4 * z))
+        mm(4 + h, "vq", "vp", 0, "oq", "op", a, z)
+        act(R("ys", a, z), bank(4 + h, 0, 160))
+        dma("s", lambda a=a, z=z: T.y[:, a:z], lambda a=a, z=z: T.ys[:, a:z], [R("ys", a, z)], [], 2.0)
+        dma("y", lambda a=a, z=z: T.oc[:, 4 * a:4 * z], lambda a=a, z=z: T.oq[:, a:z].bitcast(dt.uint8), [R("oq", a, z)], [], 2.0)
+    for k in range(4):
+        dma("y", lambda k=k: T.osc[4 * k:4 * k + 4, 0:C], lambda k=k: T.op[32 * k:32 * k + 4, 0:C], [R("op", 0, 320)], [], 2.0)
+    return ops, eng
+
+
+def links(ops):
+    seen, pred = {}, []
+    for k, o in enumerate(ops):
+        ps = set()
+        if o["after"] is not None:
+            ps.add(o["after"])
+        acc = [(r[0], bits(r), r[0] == "ps") for r in o["rd"]] + [(r[0], bits(r), True) for r in o["wr"]]
+        for name, m, w in acc:
+            for j, mj, wj in seen.get(name, []):
+                if j != k and (w or wj) and m & mj:
+                    ps.add(j)
+        for name, m, w in acc:
+            seen.setdefault(name, []).append((k, m, w))
+        pred.append(sorted(ps))
+    return pred
+
+
+def schedule(ops, pred):
+    n = len(ops)
+    E, c, l = [o["e"] for o in ops], [o["cost"] for o in ops], [o["lat"] for o in ops]
+    pf, pb = [[] for o in ops], [[] for o in ops]
+    for k in range(n):
+        for j in pred[k]:
+            d = l[j] + (0.0 if E[k] == "a" else OPT["near"] if E[j] == E[k] else OPT["far"])
+            pf[k].append((j, d))
+            pb[j].append((k, d))
+
+    def place(key, P, t0):
+        busy, end = {e: ([], []) for e in ENG}, [None] * n
+        def put(k):
+            t = t0[k]
+            for j, d in P[k]:
+                if end[j] is None:
+                    put(j)
+                if end[j] + d > t:
+                    t = end[j] + d
+            if E[k] != "a":
+                S, Z = busy[E[k]]
+                i = len(Z)
+                while i and Z[i - 1] > t:
+                    i -= 1
+                while i < len(S) and t + c[k] > S[i] + 1e-9:
+                    t = Z[i]
+                    i += 1
+                S.insert(i, t)
+                Z.insert(i, t + c[k])
+            end[k] = t + c[k]
+        for k in sorted(range(n), key=lambda k: -key[k]):
+            if end[k] is None:
+                put(k)
+        return end
+
+    zero, cur, best, now, rnd = [0.0] * n, [0.0] * n, None, None, OPT["seed"]
+    for k in range(n - 1, -1, -1):
+        cur[k] = c[k] + 1e-6 + max([cur[j] + d for j, d in pb[k]] + [l[k]])
+    for it in range(OPT["iters"]):
+        key = cur[:]
+        rnd = (rnd * 1103515245 + 12345) % 2147483648
+        kind = (rnd >> 8) % 8
+        for r in range(1 + (rnd >> 12) % 3 if it else 0):
+            rnd = (rnd * 1103515245 + 12345) % 2147483648
+            k = (rnd >> 8) % n
+            rnd = (rnd * 1103515245 + 12345) % 2147483648
+            u = rnd / 2147483648.0 - 0.5
+            key[k] += u * abs(u) * (24.0 if kind < 4 else 3.0)
+        e = place(key, pf, zero)
+        if kind == 7:
+            e = place(place([e[k] + l[k] for k in range(n)], pb, l), pf, zero)
+        m = max(e[k] + l[k] for k in range(n))
+        w = m + OPT["mean"] * sum(e) / n
+        rnd = (rnd * 1103515245 + 12345) % 2147483648
+        if now is None or w <= now + OPT["heat"] * (1.0 - it / OPT["iters"]) * (rnd / 2147483648.0) ** 4:
+            now, cur = w, [c[k] - e[k] for k in range(n)]
+        if best is None or m < best[0]:
+            best = (m, e)
+    start = [best[1][k] - c[k] for k in range(n)]
+    return sorted(range(n), key=lambda k: (start[k], k)), start, [best[1][k] + l[k] for k in range(n)]
+
+
+def rank_program(g, core, T, topo):
+    rank = T.rank_of(core)
+    if rank is None:
+        return
+    ops, eng = build(g, core, T, topo, rank)
+    pred = links(ops)
+    if "order" not in KEPT:
+        KEPT["order"] = schedule(ops, pred)
+    seq, start, done = KEPT["order"]
+    count = {e: 0 for e in ENG}
+    know = {e: {} for e in ENG}
+    mark, clock, total, nd = {}, {}, {}, [0]
+    for k in seq:
+        o = ops[k]
+        if o["kind"] == "a":
+            mark[k], clock[k] = (o["sem"], o["cnt"]), {o["sem"]: o["cnt"]}
+            total[o["sem"]] = o["cnt"]
+            continue
+        e = o["e"]
+        need = {}
+        for j in pred[k]:
+            s, n = mark[j]
+            if n > need.get(s, (0, 0))[0]:
+                need[s] = (n, j)
+        for s, (n, j) in sorted(need.items(), key=lambda x: -done[x[1][1]]):
+            if know[e].get(s, 0) < n:
+                eng[e].wait_ge(T.sem[s], n)
+                for s2, n2 in clock[j].items():
+                    know[e][s2] = max(know[e].get(s2, 0), n2)
+        ins = o["fn"]()
+        if o["kind"] == "c":
+            count[e] += 1
+            mark[k] = ("e" + e, count[e])
+            ins.then_inc(T.sem["e" + e], 1)
+        elif o["kind"] == "d":
+            mark[k] = ("d%d" % nd[0], 16)
+            nd[0] += 1
+            ins.then_inc(T.sem[mark[k][0]], 16)
+        else:
+            total["sent"] = total.get("sent", 0) + o["cnt"]
+            continue
+        total[mark[k][0]] = mark[k][1]
+        clock[k] = dict(know[e])
+        clock[k][mark[k][0]] = mark[k][1]
+    for s, n in sorted(total.items()):
+        if know["y"].get(s, 0) < n:
+            g.sync.wait_ge(T.sem[s], n)

@@ -10,8 +10,9 @@ DWS = 1120
 XH1, XH0, XX, XH2 = 0, 640, 1280, 2624
 UNIT = 1.0 / 2048
 BIG = 1e27
-OPT = {"seed": 2, "iters": 20000, "mean": 0.2, "heat": 0.15, "cut": 7, "z": "dv", "last": "ssssvsvv", "e2": "vsss",
-       "xat": 1, "eat": 0, "near": 0.07, "far": 0.1}
+OPT = {"seed": 2, "iters": 14000, "mean": 0.1, "heat": 0.15, "cut": 6, "z": "dv", "last": "ssssvsvv", "e2": "vsss",
+       "xat": 1, "eat": 0, "near": 0.17, "far": 0.18, "osc": "ysys"}
+CASES = [(0.2, 0.2, 0.08, 0.5, 0.0, 0.9), (0.15, 0.15, 0.1, 1.0, 1.0, 0.9)]
 
 SCRATCH = {
     "xt": ("sbuf", [128, 1344], B), "ut": ("sbuf", [128, 512], B), "vt": ("sbuf", [128, 512], B),
@@ -28,7 +29,7 @@ SCRATCH = {
     "be": ("sbuf", [128, 1088], B), "beq": ("sbuf", [128, 272], Q), "bep": ("sbuf", [128, 272], P),
     "pbq": ("sbuf", [128, 144], Q), "pbp": ("sbuf", [128, 144], P),
     "lt": ("sbuf", [128, 512], B),
-    "l1q": ("sbuf", [128, 144], Q), "l1p": ("sbuf", [128, 192], P),
+    "l1q": ("sbuf", [128, 160], Q), "l1p": ("sbuf", [128, 256], P),
     "l2q": ("sbuf", [128, 160], Q), "l2p": ("sbuf", [128, 256], P),
     "zf": ("sbuf", [128, 512], B), "zfq": ("sbuf", [128, 256], Q), "zfp": ("sbuf", [128, 256], P),
     "ef": ("sbuf", [128, 320], B), "tf": ("sbuf", [128, 128], F),
@@ -40,22 +41,22 @@ SCRATCH = {
     "ps": ("psum", [128, 4096], F),
     "lraw": ("sbuf", [128, 44], I), "li": ("sbuf", [128, 256], I), "sm": ("sbuf", [128, 1024], F),
     "of": ("sbuf", [128, 512], U), "uo": ("sbuf", [128, 8], U),
-    "tin": ("sbuf", [128, 704], F), "win": ("sbuf", [128, 1408], F),
+    "tin": ("sbuf", [128, 704], F), "win": ("sbuf", [128, 2080], F), "sw": ("sbuf", [128, 192], F),
     "gg": ("sbuf", [128, 896], F), "tt": ("sbuf", [128, 896], F),
     "io16": ("sbuf", [128, 160], B), "m16": ("sbuf", [128, 160], B), "k16": ("sbuf", [128, 160], B),
     "sc1": ("sbuf", [128, 480], F), "sc2": ("sbuf", [128, 480], F),
     "ones": ("sbuf", [128, 252], B), "sig": ("sbuf", [128, 402], B),
     "thr": ("sbuf", [128, 756], F), "k21": ("sbuf", [128, 252], B),
-    "ko": ("sbuf", [128, 48], F), "snd": ("sbuf", [128, 60], F),
-    "msg0": ("sbuf", [128, 32], F), "msg1": ("sbuf", [128, 32], F), "msg2": ("sbuf", [128, 32], F),
+    "ko": ("sbuf", [128, 48], F), "snd": ("sbuf", [128, 96], F),
+    "msg0": ("sbuf", [128, 44], F), "msg1": ("sbuf", [128, 44], F), "msg2": ("sbuf", [128, 44], F),
     "yy": ("sbuf", [128, 1008], F), "cc": ("sbuf", [128, 1296], B), "cs": ("sbuf", [128, 1200], B),
     "cw": ("sbuf", [128, 96], F), "mm": ("sbuf", [128, 848], F), "ms": ("sbuf", [128, 848], F),
     "lab": ("sbuf", [128, 432], F), "ws_": ("sbuf", [128, 1104], F), "wt": ("sbuf", [128, 640], F),
-    "oi": ("sbuf", [128, 64], F), "ot": ("sbuf", [128, 64], F),
+    "oi": ("sbuf", [128, 64], F), "ot": ("sbuf", [128, 64], F), "od": ("dram", [16, 512], F),
 }
 ENG = ["v", "s", "p", "g", "y"]
-ARR = ["ax", "axs", "ab", "abs_", "ak0", "ak1", "ak2", "al1", "al2"]
-SEMAPHORES = ["e" + k for k in ENG] + ARR + ["sent"] + ["d%d" % k for k in range(48)]
+ARR = ["ax", "axs", "ab", "abs_", "ak0", "ak1", "ak2", "al1", "al2", "as1", "as2"]
+SEMAPHORES = ["e" + k for k in ENG] + ARR + ["sent"] + ["d%d" % k for k in range(32)]
 WIDTH = {F: 4, B: 2, I: 4, U: 2, Q: 4, P: 1}
 CYC = 0.001
 GAT = 1.6
@@ -182,7 +183,7 @@ def build(g, core, T, topo, rank):
             if acc:
                 return g.dma_start(out(), in_(), accum_op=A.add)
             return eng[e].dma_start(out(), in_())
-        add(e, fn, rd, wr, 0.9 if e == "g" else 0.08, "d", lat)
+        add(e, fn, rd, wr, 0.9 if e == "g" else 0.1, "d", lat)
 
     def accumulate(out, in_):
         dma("g", lambda: ap(out), lambda: ap(in_), [in_, out], [out], 2.5, True)
@@ -193,18 +194,18 @@ def build(g, core, T, topo, rank):
     def mask(es):
         return sum(1 << e for e in es)
 
-    def send(peer, pairs, sem, part, lat):
+    def send(peer, items, part):
         rid, pid = topo.addr(peer)[:2]
         es = part(topo.engines(core, peer))
         def fn():
-            if len(pairs) == 1:
-                return g.remote_dma(u8(pairs[0][1]), u8(pairs[0][0]), T.sem[sem], T.sem.sent, pid, rid, mask(es[0]))
+            if len(items) == 1:
+                return g.remote_dma(u8(items[0][1]), u8(items[0][0]), T.sem[items[0][2]], T.sem.sent, pid, rid, mask(es[0]))
             return g.remote_dma_fused([RemoteDMATransfer(dst_ids=[DstId(rid=rid, pnc=pid)], dma_engine_mask=mask(es[k]),
-                                                         remote_sem=T.sem[sem], src=u8(pairs[k][0]), dst=u8(pairs[k][1]))
-                                       for k in range(len(pairs))], local_sem=T.sem.sent)
-        n = sum(len(e) for e in es)
-        k = add("g", fn, [p[0] for p in pairs], [], 0.5, "r", cnt=n)
-        add("a", None, [], [p[1] for p in pairs], 0.0, "a", lat, k, sem, n)
+                                                         remote_sem=T.sem[x[2]], src=u8(x[0]), dst=u8(x[1]))
+                                       for k, x in enumerate(items)], local_sem=T.sem.sent)
+        k = add("g", fn, [x[0] for x in items], [], 0.7, "r", cnt=sum(len(e) for e in es))
+        for x, e in zip(items, es):
+            add("a", None, [], [x[1]], 0.0, "a", x[3], k, x[2], len(e))
 
     free = {"sm": 0, "of": 0, "li": 0}
 
@@ -223,9 +224,8 @@ def build(g, core, T, topo, rank):
     low = [rank < (rank ^ s) for s in STEP]
     first = [0 if l else SL for l in low]
     pfirst = [SL - f for f in first]
-    chip = [topo.chip(core) == topo.chip(p) for p in peer]
     allE = lambda es: [es]
-    if_on = lambda t, on, off: on if chip[t] else off
+    three = lambda es: [es[len(es) // 2:], es[:len(es) // 4], es[len(es) // 4:len(es) // 2]]
 
     dma("y", lambda: T.lraw[:, 0:20], lambda: T.ri[:], [], [R("lraw", 0, 20)], 1.9)
     dma("s", lambda: T.lraw[:, 40:41], lambda: T.ro[:], [], [R("lraw", 40, 41)], 1.9)
@@ -258,6 +258,7 @@ def build(g, core, T, topo, rank):
         quant("eq", "ep", 128 * b, 128 * b + 128, R("ec", 3 - b, 515 - b))
     iota(R("zf", 0, 512), [[0, 512]], 0, 0)
     iota(R("lt", 0, 512), [[0, 512]], 0, 0)
+    iota(R("snd", 0, 96), [[0, 96]], 0, 0)
     mset(R("xt", 1280, 1344), 0.0)
     mset(R("dw", 1104, 4 * DWS, DWS), 0.0)
     mset(R("cw", 20, 96, 32), 0.0)
@@ -301,6 +302,10 @@ def build(g, core, T, topo, rank):
     asel(R("sig", 1, 201), R("ones", 0, 200), [[-1, 10], [1, 10], [0, 2]], A.is_ge, -1.0, 0, 0)
     asel(R("sig", 201, 401), R("ones", 0, 200), [[1, 10], [-1, 10], [0, 2]], A.is_gt, -1.0, 0, 0)
     mset(R("sig", 0, 400, 20), 0.0)
+    yi, oy = new("li", 4), new("of", 4)
+    iota(yi, [[16, 2], [0, 2]], 0, 0)
+    ts(oy, yi, mcol, None, A.add)
+    ts(R("sw", 0, 32), R("ones", 0, 32), h16, 639.0, A.add, A.add)
 
     t41, pv = new("li", 41), new("sm", 41)
     ts(t41, R("lraw", 0, 41), 496, None, A.bitwise_and)
@@ -308,30 +313,47 @@ def build(g, core, T, topo, rank):
     for o in (0, 16):
         ts(R("tin", o, 640, 32), sub(pv, 0, 20), h16, None, A.add)
     ts(R("tin", 672, 704, 16), zz, sub(pv, 40, 41), h16, A.add, A.add)
-    tr(R("win", 0, 704), R("tin", 0, 704))
+    WL, WR, W12 = R("win", 0, 704), R("win", 704, 1408), R("win", 704, 2080)
+    tr(WR, R("tin", 0, 704))
+    lin(R("sw", 0, 20), sub(pv, 0, 20), 1.0, h16)
+    tr(R("sw", 32, 64), R("sw", 0, 32))
+    gat("s", R("sw", 64, 128), R("sw", 32, 64), oy)
+    tr(R("sw", 128, 192), R("sw", 64, 128))
+    o2 = new("of", 42)
+    cp(sub(o2, 0, 42, 2), R("sw", 128, 149))
+    cp(sub(o2, 1, 42, 2), R("sw", 160, 181))
+    gat("s", R("win", 1408, 1760), WR, sub(o2, 0, 22))
+    gat("v", R("win", 1760, 1920), WR, sub(o2, 22, 32))
+    gat("v", R("win", 1920, 2080), WR, sub(o2, 32, 42))
     for o in (0, 16):
         lin(R("tin", o, 640, 32), sub(pv, 20, 40), 1.0, h16)
-    for k in range(11):
-        tr(R("win", 704 + 64 * k, 768 + 64 * k), R("tin", 64 * k, 64 * k + 64))
+    for k in range(6):
+        tr(R("win", 128 * k, min(128 * k + 128, 704)), R("tin", 128 * k, min(128 * k + 128, 704)))
     quant("xq", "xp", 0, 160, R("xt", 0, 640))
     quant("xq", "xp", 160, 336, R("xt", 640, 1344))
-    WR, WL = R("win", 0, 704), R("win", 704, 1408)
-    oc0, oc1 = new("of", 18), new("of", 32)
-    for i in range(SL):
-        gat("v", R("gg", 32 * i, 32 * i + 32), WR, oroot if i == 0 else sub(oc0, 2 * i - 2, 2 * i))
-        if i == OPT["xat"]:
+    oc0 = new("of", 6)
+
+    def step(e, a, n, w, o):
+        gat(e, R("gg", a, a + n), w, o)
+        if a == 32 * OPT["xat"]:
             ops[-1]["rd"].append(R("xp", 0, 336))
-        if i == OPT["eat"]:
+        if a == 32 * OPT["eat"]:
             ops[-1]["rd"].append(R("ep", 0, 512))
-        tr(R("tt", 32 * i, 32 * i + 32), R("gg", 32 * i, 32 * i + 32))
-        if i < SL - 1:
-            cp(sub(oc0, 2 * i, 2 * i + 2), R("tt", 32 * i, 32 * i + 32, 16))
-    for s in range(9):
-        a = 320 + 64 * s
-        gat("s", R("gg", a, a + 64), WL if s == 0 else WR, sub(oc0, 0, 4) if s == 0 else sub(oc1, 4 * s - 4, 4 * s))
-        tr(R("tt", a, a + 64), R("gg", a, a + 64))
-        if s < 8:
-            cp(sub(oc1, 4 * s, 4 * s + 4), R("tt", a, a + 64, 16))
+        tr(R("tt", a, a + n), R("gg", a, a + n))
+
+    def both(o, a, n):
+        cp(sub(o, 0, n // 16), R("tt", a, a + n, 16))
+        ts(sub(o, n // 16, n // 8), R("tt", a, a + n, 16), 704.0, None, A.add)
+        return o
+
+    step("v", 0, 32, WR, oroot)
+    cp(sub(oc0, 0, 2), R("tt", 0, 32, 16))
+    step("v", 32, 32, WR, sub(oc0, 0, 2))
+    for i in (1, 3, 5, 7):
+        step("v", 32 * i + 32, 64, W12, both(sub(oc0, 2, 6) if i == 1 else new("of", 4), 32 * i, 32))
+    step("s", 320, 64, WL, sub(oc0, 0, 4))
+    for s in (0, 2, 4, 6):
+        step("s", 384 + 64 * s, 128, W12, both(new("of", 8), 320 + 64 * s, 64))
 
     def places(pos, out):
         n = size(pos)
@@ -344,8 +366,8 @@ def build(g, core, T, topo, rank):
     CR = [sub(CA, 12 * t, 12 * t + 12) for t in range(3)]
     mset(sub(CA, 10, 36, 12), float(C))
 
-    send(peer[0], [(R("xq", 0, 320), R("pxq", 0, 320))], "ax", allE, 2.5)
-    send(peer[0], [(R("xp", 0, 320), R("pxp", 0, 320))], "axs", allE, 2.5)
+    send(peer[0], [(R("xq", 0, 320), R("pxq", 0, 320), "ax", 2.8)], allE)
+    send(peer[0], [(R("xp", 0, 320), R("pxp", 0, 320), "axs", 2.8)], allE)
     for b in range(4):
         act(R("xw", XX + 336 * b, XX + 336 * b + 336), R("xt", b, 1344, 4), AF.Copy, 0.5)
     quant("uq", "up", 0, 128, R("ut", 0, 512))
@@ -378,8 +400,8 @@ def build(g, core, T, topo, rank):
         return R("sc2", at + 15, at + n, 16)
 
     KO = [R("ko", 16 * t, 16 * t + 10) for t in range(3)]
-    SK = [R("snd", 20 * t, 20 * t + 10) for t in range(3)]
-    SB = [R("snd", 20 * t + 10, 20 * t + 20) for t in range(3)]
+    SK = [R("snd", 32 * t, 32 * t + 10) for t in range(3)]
+    SB = [R("snd", 32 * t + 22, 32 * t + 32) for t in range(3)]
     MS = ["msg0", "msg1", "msg2"]
     cap, ncap, nl, e4, kn = [], [], [], [], []
     ZC = [640, 928, 816]
@@ -396,7 +418,7 @@ def build(g, core, T, topo, rank):
         late = OWN[t][2]
         ce = new("sm", 10)
         tt(ce, c, ne, A.add)
-        for (dst, k, (cx, cl, _)) in ((SB[t], 20.0 - pfirst[t], PAR[t]), (R(MS[t], 20, 30), 10.0 - first[t], OWN[t])):
+        for (dst, k, (cx, cl, _)) in ((SB[t], 20.0 - pfirst[t], PAR[t]), (R(MS[t], 32, 42), 10.0 - first[t], OWN[t])):
             if cx is None:
                 lin(sub(dst, late, 10), sub(qe, late, 10), UNIT, k - 16 * UNIT)
             else:
@@ -405,19 +427,18 @@ def build(g, core, T, topo, rank):
                 lin(sub(dst, 0, late), sub(qe, 0, late), UNIT, k + cl * UNIT)
         lin(e4[t], c, 4.0, -4.0 * (C - 1), AF.Relu)
         iota(kn[t], [[-1, 10]], -1 - first[t], 0)
-        lin(nl[t], sub(CR[t], 1, 11), -8.0, 8.0 * C)
+        lin(nl[t], sub(CR[t], 1, 11), -16384.0, 16384.0 * C)
 
     def keys(t, s, a, b):
         tt(sub(SK[t], a, b), s, sub(ncap[t], a, b), A.max if low[t] else A.min)
         tt(sub(KO[t], a, b), s, sub(cap[t], a, b), A.min)
 
-    def send_keys(t):
-        send(peer[t], [(R("snd", 20 * t, 20 * t + 20), R(MS[t], 0, 20))], "ak%d" % t,
-             if_on(t, lambda es: [es[len(es) // 2:]], allE), 1.6)
+    def note(t):
+        return (R("snd", 32 * t, 32 * t + 32), R(MS[t], 0, 32), "ak%d" % t, 2.0)
 
     tables(0)
     keys(0, diag(4, 160, 0), 0, 10)
-    send_keys(0)
+    send(peer[0], [note(0)], allE)
     decode("pxq", "pxp", 320, 288, 0)
 
     c12 = new("sm", 18)
@@ -433,8 +454,8 @@ def build(g, core, T, topo, rank):
         gat("s", R("be", 576 + b, 1088, 4), xwin(b), ob2, 2.0)
     quant("beq", "bep", 0, 144, R("be", 0, 576))
     quant("beq", "bep", 144, 272, R("be", 576, 1088))
-    send(peer[1], [(R("beq", 0, 144), R("pbq", 0, 144))], "ab", allE, 2.5)
-    send(peer[1], [(R("bep", 0, 144), R("pbp", 0, 144))], "abs_", allE, 2.5)
+    send(peer[1], [(R("beq", 0, 144), R("pbq", 0, 144), "ab", 2.8)], allE)
+    send(peer[1], [(R("bep", 0, 144), R("pbp", 0, 144), "abs_", 2.8)], allE)
     mm(5, "u2q", "u2p", 0, "beq", "bep", 0, 144)
     tables(1); tables(2)
     keys(1, diag(5, 144, 160), 1, 10)
@@ -492,11 +513,10 @@ def build(g, core, T, topo, rank):
         tt(R("oi", 0, 20), d, R("lraw", 0, 20), A.add)
         tt(R("oi", 32, 52), R("lraw", 20, 40), d, A.subtract)
         tr(R("ot", 0, 64), R("oi", 0, 64))
-        for gr in range(8):
-            for s in range(2):
-                p0, c0 = 32 * (gr // 2), 32 * s + 16 * (gr % 2)
-                dma("y", lambda gr=gr, s=s: T.ol[gr:gr + 1, C * s:C * s + C], lambda p0=p0, c0=c0: T.ot[p0:p0 + 20, c0:c0 + 16],
-                    [R("ot", 0, 64)], [], 2.0)
+        for k in range(4):
+            dma("y", lambda k=k: T.od[k:16:4, :], lambda k=k: T.ot[:, 32 * (k % 2) + 16 * (k // 2):32 * (k % 2) + 16 * (k // 2) + 16],
+                [R("ot", 0, 64)], [R("od", k, k + 1)], 2.2)
+        dma("y", lambda: T.ol[:], lambda: T.od[:, 0:C], [R("od", 0, 4)], [], 2.2)
         return out
 
     def order(t):
@@ -512,27 +532,27 @@ def build(g, core, T, topo, rank):
         tt(R("cc", c0 + 1, c0 + 224, 2), PK, Y[2], A.is_ge, omn)
         scan(R("thr", 252 * t + 41, 252 * t + 232, 21), kn[t], e4[t], A.add, A.subtract, 1000.0)
         scan(R("cs", s0, s0 + 400), R("sig", 0, 400), R("cc", c0 + 24, c0 + 424), A.mult, A.add)
-        tt(R("cw", 32 * t, 32 * t + 20), R(MS[t], 10, 30), R("cs", s0 + 19, s0 + 400, 20), A.subtract)
+        tt(R("cw", 32 * t, 32 * t + 20), R(MS[t], 22, 42), R("cs", s0 + 19, s0 + 400, 20), A.subtract)
 
     DF = new("sm", 36)
     mset(sub(DF, 10, 36, 12), 4.0)
 
-    def sources(t, at, n, k):
+    def sums(t, at, n):
         tt(R("mm", at, at + n), R("cw", 32 * t, 32 * t + 21), R("thr", 252 * t, 252 * t + n), A.max, sub(oseg, 0, n // 16))
         scan(R("ms", at, at + n), R("k21", 0, n), R("mm", at, at + n), A.mult, A.add)
-        df = sub(DF, 12 * t, 12 * t + 11) if k == 10 else new("sm", k + 1)
-        tt(sub(df, 0, k), R("ms", at + 20, at + 21 * k, 21), R("ms", at + 41, at + 21 * k + 21, 21), A.subtract)
-        return df
 
     def dwin(t, b):
         return R("dw", DWS * b + WIN[t][0], DWS * b + WIN[t][1])
 
     def fast(t):
-        df = sources(t, 720 + 64 * t, 64, 2)
-        oa, on, nf = new("of", 1), new("of", 1), new("sm", 1)
-        ts(oa, sub(df, 0, 1), 2048.0, None, A.mult)
-        ts(nf, sub(df, 0, 1), sub(nl[t], 0, 1), sub(df, 1, 2), A.add, A.min)
-        ts(on, nf, 2048.0, None, A.mult)
+        at = 720 + 64 * t
+        sums(t, at, 64)
+        G = [R("ms", at + 20 + 21 * i, at + 21 + 21 * i) for i in range(3)]
+        oa, on, d0, d1 = new("of", 1), new("of", 1), new("sm", 1), new("sm", 1)
+        ts(oa, G[0], G[1], 2048.0, A.subtract, A.mult)
+        ts(d0, G[0], G[1], 2048.0, A.subtract, A.mult)
+        ts(d1, G[1], G[2], 2048.0, A.subtract, A.mult)
+        ts(on, d0, sub(nl[t], 0, 1), d1, A.add, A.min)
         e0 = 128 * t
         for b in range(4):
             gat("s", R("ef", e0 + b, e0 + 64, 4), dwin(t, b), oa)
@@ -543,11 +563,8 @@ def build(g, core, T, topo, rank):
             mm(b, "wq", "wp", 128 * b, "zfq", "zfp", 128 * t, 128 * t + 128)
             act(R("tf", 64 * t + b, 64 * t + 64, 4), bank(b, 0, 16), AF.Relu, 0.03125)
         tt(R("lt", 0, 64), R("tf", 64 * t, 64 * t + 64), R("ef", e0 + 64, e0 + 128), A.add)
-        qn, pn, n = ("l1q", "l1p", 16) if t == 0 else ("l2q", "l2p", 32)
+        qn, pn = ("l1q", "l1p") if t == 0 else ("l2q", "l2p")
         quant(qn, pn, 0, 128, R("lt", 0, 512))
-        send(peer[t + 1], [(R(qn, 0, n), R(qn, 128, 128 + n)), (R(pn, 0, 4 * n), R(pn, 128, 128 + 4 * n))], "al%d" % (t + 1),
-             if_on(t + 1, lambda es: [es[:len(es) // 4], es[len(es) // 4:len(es) // 2]],
-                   lambda es: [es[:len(es) // 2], es[len(es) // 2:]]), 2.0)
         mm(4, "u2q", "u2p", 0, qn, pn, 0, 128)
         if t == 0:
             tt(R("sc1", 432, 448), bank(4, 0, 16), R("m16", 0, 16), A.mult)
@@ -555,10 +572,14 @@ def build(g, core, T, topo, rank):
             red(sub(KO[1], 0, 1), R("sc1", 432, 448))
         else:
             keys(2, diag(4, 32, 448), 0, 2)
-        send_keys(t + 1)
+        send(peer[t + 1], [note(t + 1), (R(qn, 0, 32), R(qn, 128, 160), "al%d" % (t + 1), 2.5),
+                           (R(pn, 0, 128), R(pn, 128, 256), "as%d" % (t + 1), 2.5)], three)
 
     def full(t):
-        df = sources(t, 240 * t, 240, 10)
+        at = 240 * t
+        sums(t, at, 240)
+        df = sub(DF, 12 * t, 12 * t + 11)
+        tt(sub(df, 0, 10), R("ms", at + 20, at + 210, 21), R("ms", at + 41, at + 231, 21), A.subtract)
         oa, on, nf = new("of", 10), new("of", 10), new("sm", 10)
         ts(oa, sub(df, 0, 10), 2048.0, float(ZC[t]), A.mult, A.min)
         tt(nf, sub(df, 0, 10), nl[t], A.add)
@@ -619,10 +640,10 @@ def build(g, core, T, topo, rank):
         quant("oq", "op", a, z, R("xo", 4 * a, 4 * z))
         mm(4 + h, "vq", "vp", 0, "oq", "op", a, z)
         act(R("ys", a, z), bank(4 + h, 0, 160))
-        dma("s", lambda a=a, z=z: T.y[:, a:z], lambda a=a, z=z: T.ys[:, a:z], [R("ys", a, z)], [], 2.0)
-        dma("y", lambda a=a, z=z: T.oc[:, 4 * a:4 * z], lambda a=a, z=z: T.oq[:, a:z].bitcast(dt.uint8), [R("oq", a, z)], [], 2.0)
+    dma("s", lambda: T.y[:], lambda: T.ys[:], [R("ys", 0, C)], [], 2.1)
+    dma("y", lambda: T.oc[:], lambda: T.oq[:].bitcast(dt.uint8), [R("oq", 0, C)], [], 2.1)
     for k in range(4):
-        dma("y", lambda k=k: T.osc[4 * k:4 * k + 4, 0:C], lambda k=k: T.op[32 * k:32 * k + 4, 0:C], [R("op", 0, 320)], [], 2.0)
+        dma(OPT["osc"][k], lambda k=k: T.osc[4 * k:4 * k + 4, 0:C], lambda k=k: T.op[32 * k:32 * k + 4, 0:C], [R("op", 0, C)], [], 1.9)
     return ops, eng
 
 
@@ -652,6 +673,27 @@ def schedule(ops, pred):
             d = l[j] + (0.0 if E[k] == "a" else OPT["near"] if E[j] == E[k] else OPT["far"])
             pf[k].append((j, d))
             pb[j].append((k, d))
+    cases = []
+    for (near, far, di, ra, rl, cf) in CASES:
+        cc = [di if o["kind"] == "d" and o["e"] != "g" else ra if o["kind"] == "r" else o["cost"] * cf if o["kind"] == "c" else o["cost"] for o in ops]
+        ll = [o["lat"] + (rl - 0.4 if o["kind"] == "a" else 0.0) for o in ops]
+        cases.append((cc, ll, [[(j, 0.0 if E[k] == "a" else near if E[j] == E[k] else far) for j in pred[k]] for k in range(n)]))
+
+    def replay(seq):
+        out = []
+        for cc, ll, pp in cases:
+            fr, dn = {e: 0.0 for e in ENG}, [0.0] * n
+            for k in seq:
+                t = fr.get(E[k], 0.0)
+                for j, d in pp[k]:
+                    if dn[j] + d > t:
+                        t = dn[j] + d
+                t += cc[k]
+                if E[k] != "a":
+                    fr[E[k]] = t
+                dn[k] = t + ll[k]
+            out.append(max(dn))
+        return out
 
     def place(key, P, t0):
         busy, end = {e: ([], []) for e in ENG}, [None] * n
@@ -694,15 +736,16 @@ def schedule(ops, pred):
         e = place(key, pf, zero)
         if kind == 7:
             e = place(place([e[k] + l[k] for k in range(n)], pb, l), pf, zero)
-        m = max(e[k] + l[k] for k in range(n))
+        seq = sorted(range(n), key=lambda k: (e[k] - c[k], k))
+        times = replay(seq)
+        m = sum(times) / len(times)
         w = m + OPT["mean"] * sum(e) / n
         rnd = (rnd * 1103515245 + 12345) % 2147483648
         if now is None or w <= now + OPT["heat"] * (1.0 - it / OPT["iters"]) * (rnd / 2147483648.0) ** 4:
             now, cur = w, [c[k] - e[k] for k in range(n)]
         if best is None or m < best[0]:
-            best = (m, e)
-    start = [best[1][k] - c[k] for k in range(n)]
-    return sorted(range(n), key=lambda k: (start[k], k)), start, [best[1][k] + l[k] for k in range(n)]
+            best = (m, seq, [e[k] + l[k] for k in range(n)], times)
+    return best[1], best[3], best[2]
 
 
 def rank_program(g, core, T, topo):
@@ -713,7 +756,7 @@ def rank_program(g, core, T, topo):
     pred = links(ops)
     if "order" not in KEPT:
         KEPT["order"] = schedule(ops, pred)
-    seq, start, done = KEPT["order"]
+    seq, times, done = KEPT["order"]
     count = {e: 0 for e in ENG}
     know = {e: {} for e in ENG}
     mark, clock, total, nd = {}, {}, {}, [0]

from concourse.bass import DstId, RemoteDMATransfer
from concourse.mybir import dt, AluOpType, AxisListType, ActivationFunctionType

A = AluOpType
AF = ActivationFunctionType
C, TR, SL = 320, 16, 10
STEP = [1, 2, 1]
F, B, I, U, Q, P = "float32", "bfloat16", "int32", "uint16", "float8_e4m3fn_x4", "uint8"
DWS = 1120
XH1, XH0, XX, XH2 = 0, 640, 1280, 2624
UNIT = 1.0 / 2048
BIG = 1e27
OPT = {"seed": 2, "iters": 14000, "mean": 0.1, "heat": 0.15, "cut": 6, "z": "dv", "last": "ssssvsvv", "e2": "vsss",
       "xat": 1, "eat": 0, "near": 0.17, "far": 0.18, "osc": "ysys"}
CASES = [(0.2, 0.2, 0.08, 0.5, 0.0, 0.9), (0.15, 0.15, 0.1, 1.0, 1.0, 0.9)]

SCRATCH = {
    "xt": ("sbuf", [128, 1344], B), "ut": ("sbuf", [128, 512], B), "vt": ("sbuf", [128, 512], B),
    "wq": ("sbuf", [128, 512], Q), "wp": ("sbuf", [128, 512], P),
    "uq": ("sbuf", [128, 128], Q), "up": ("sbuf", [128, 128], P),
    "u2q": ("sbuf", [128, 128], Q), "u2p": ("sbuf", [128, 128], P),
    "vq": ("sbuf", [128, 128], Q), "vp": ("sbuf", [128, 128], P),
    "xq": ("sbuf", [128, 336], Q), "xp": ("sbuf", [128, 336], P),
    "pxq": ("sbuf", [128, 320], Q), "pxp": ("sbuf", [128, 320], P),
    "half": ("sbuf", [128, 516], B), "ec": ("sbuf", [128, 516], B),
    "eq": ("sbuf", [128, 512], Q), "ep": ("sbuf", [128, 512], P),
    "xw": ("sbuf", [128, 3264], F), "dw": ("sbuf", [128, 4 * DWS], B),
    "b0": ("sbuf", [128, 640], B), "b0q": ("sbuf", [128, 160], Q), "b0p": ("sbuf", [128, 160], P),
    "be": ("sbuf", [128, 1088], B), "beq": ("sbuf", [128, 272], Q), "bep": ("sbuf", [128, 272], P),
    "pbq": ("sbuf", [128, 144], Q), "pbp": ("sbuf", [128, 144], P),
    "lt": ("sbuf", [128, 512], B),
    "l1q": ("sbuf", [128, 160], Q), "l1p": ("sbuf", [128, 256], P),
    "l2q": ("sbuf", [128, 160], Q), "l2p": ("sbuf", [128, 256], P),
    "zf": ("sbuf", [128, 512], B), "zfq": ("sbuf", [128, 256], Q), "zfp": ("sbuf", [128, 256], P),
    "ef": ("sbuf", [128, 320], B), "tf": ("sbuf", [128, 128], F),
    "eh": ("sbuf", [128, 1920], B), "zt": ("sbuf", [128, 1920], B),
    "zq": ("sbuf", [128, 480], Q), "zp": ("sbuf", [128, 480], P),
    "t2": ("sbuf", [128, 640], F),
    "xo": ("sbuf", [128, 1280], B), "oq": ("sbuf", [128, 320], Q), "op": ("sbuf", [128, 320], P),
    "ys": ("sbuf", [128, 320], F),
    "ps": ("psum", [128, 4096], F),
    "lraw": ("sbuf", [128, 44], I), "li": ("sbuf", [128, 256], I), "sm": ("sbuf", [128, 1024], F),
    "of": ("sbuf", [128, 512], U), "uo": ("sbuf", [128, 8], U),
    "tin": ("sbuf", [128, 704], F), "win": ("sbuf", [128, 2080], F), "sw": ("sbuf", [128, 192], F),
    "gg": ("sbuf", [128, 896], F), "tt": ("sbuf", [128, 896], F),
    "io16": ("sbuf", [128, 160], B), "m16": ("sbuf", [128, 160], B), "k16": ("sbuf", [128, 160], B),
    "sc1": ("sbuf", [128, 480], F), "sc2": ("sbuf", [128, 480], F),
    "ones": ("sbuf", [128, 252], B), "sig": ("sbuf", [128, 402], B),
    "thr": ("sbuf", [128, 756], F), "k21": ("sbuf", [128, 252], B),
    "ko": ("sbuf", [128, 48], F), "snd": ("sbuf", [128, 96], F),
    "msg0": ("sbuf", [128, 44], F), "msg1": ("sbuf", [128, 44], F), "msg2": ("sbuf", [128, 44], F),
    "yy": ("sbuf", [128, 1008], F), "cc": ("sbuf", [128, 1296], B), "cs": ("sbuf", [128, 1200], B),
    "cw": ("sbuf", [128, 96], F), "mm": ("sbuf", [128, 848], F), "ms": ("sbuf", [128, 848], F),
    "lab": ("sbuf", [128, 432], F), "ws_": ("sbuf", [128, 1104], F), "wt": ("sbuf", [128, 640], F),
    "oi": ("sbuf", [128, 64], F), "ot": ("sbuf", [128, 64], F), "od": ("dram", [16, 512], F),
}
ENG = ["v", "s", "p", "g", "y"]
ARR = ["ax", "axs", "ab", "abs_", "ak0", "ak1", "ak2", "al1", "al2", "as1", "as2"]
SEMAPHORES = ["e" + k for k in ENG] + ARR + ["sent"] + ["d%d" % k for k in range(32)]
WIDTH = {F: 4, B: 2, I: 4, U: 2, Q: 4, P: 1}
CYC = 0.001
GAT = 1.6
KEPT = {}


def R(name, a, b, s=1):
    return (name, a, b, s)


def size(r):
    return len(range(r[1], r[2], r[3]))


def bits(r):
    if r[0] == "ps":
        m = 0
        for k in range(r[1] // 512, (r[2] - 1) // 512 + 1):
            m |= 1 << k
        return m
    if r[3] == 1:
        return ((1 << (r[2] - r[1])) - 1) << r[1]
    m = 0
    for k in range(r[1], r[2], r[3]):
        m |= 1 << k
    return m


def build(g, core, T, topo, rank):
    ops = []
    eng = {"v": g.vector, "s": g.scalar, "p": g.tensor, "g": g, "y": g.sync}

    def ap(r):
        if not isinstance(r, tuple):
            return r
        return T[r[0]][:, r[1]:r[2]] if r[3] == 1 else T[r[0]][:, r[1]:r[2]:r[3]]

    def ind(w, o):
        return ap(w).indirect(ap(o))

    def add(e, fn, rd, wr, cost, kind="c", lat=0.0, after=None, sem=None, cnt=0):
        ops.append({"e": e, "fn": fn, "rd": [r for r in rd if isinstance(r, tuple)], "wr": wr, "cost": cost,
                    "kind": kind, "lat": lat, "after": after, "sem": sem, "cnt": cnt})
        return len(ops) - 1

    def narrow(*rs):
        return all(WIDTH[SCRATCH[r[0]][2]] == 2 for r in rs)

    def cost(n, o=None, f=1.0):
        return CYC * (60 + GAT * n if o else max(64, n * f))

    def src(r, o):
        return ind(r, o) if o else ap(r)

    def ts(out, in0, s1, s2, op0, op1=None, o=None):
        def fn():
            if op1 is None:
                return g.vector.tensor_scalar(ap(out), src(in0, o), ap(s1), None, op0)
            return g.vector.tensor_scalar(ap(out), src(in0, o), ap(s1), ap(s2), op0, op1)
        add("v", fn, [in0, s1, s2, o], [out], cost(size(out), o, 0.5 if narrow(out, in0) else 1.0))

    def tt(out, in0, in1, op, o=None):
        f = 1.0 if "ps" in (in0[0], in1[0]) else 2.0
        add("v", lambda: g.vector.tensor_tensor(ap(out), src(in0, o), ap(in1), op), [in0, in1, o], [out], cost(size(out), o, f))

    def cp(out, in_, o=None):
        add("v", lambda: g.vector.tensor_copy(ap(out), src(in_, o)), [in_, o], [out], cost(size(out), o, 0.5 if narrow(out, in_) else 1.0))

    def act(out, in_, func=AF.Copy, scale=1.0, bias=None, o=None):
        def fn():
            if bias is not None:
                return g.scalar.activation(ap(out), src(in_, o), func, bias=ap(bias), scale=scale)
            if scale != 1.0:
                return g.scalar.activation(ap(out), src(in_, o), func, scale=scale)
            return g.scalar.activation(ap(out), src(in_, o), func)
        add("s", fn, [in_, o, bias], [out], cost(size(out), o) + 0.02)

    def lin(out, in_, scale, bias, func=AF.Identity):
        act(out, in_, func, float(scale), bias if isinstance(bias, tuple) else float(bias))

    def gat(e, out, w, o, scale=1.0):
        if e == "s":
            act(out, w, AF.Copy, scale, None, o)
        elif scale == 1.0:
            cp(out, w, o)
        else:
            ts(out, w, scale, None, A.mult, None, o)

    def scan(out, d0, d1, op0, op1, init=0.0):
        add("v", lambda: g.vector.tensor_tensor_scan(ap(out), ap(d0), ap(d1), init, op0, op1), [d0, d1], [out],
            cost(size(out), None, 0.5 if narrow(out, d0, d1) else 1.0))

    def red(out, in_):
        add("v", lambda: g.vector.tensor_reduce(ap(out), ap(in_), AxisListType.X, A.add), [in_], [out], cost(size(in_)))

    def tr(out, in_):
        add("v", lambda: g.vector.transpose(ap(out), ap(in_)), [in_], [out], cost(size(out)))

    def mset(out, val):
        add("v", lambda: g.vector.memset(ap(out), val), [], [out], cost(size(out), None, 0.5 if narrow(out) else 1.0))

    def iota(out, pat, base, ch):
        def fn():
            if SCRATCH[out[0]][2] == I:
                return g.iota(ap(out), pat, base, ch)
            return g.iota(ap(out), pat, base, ch, allow_small_or_imprecise_dtypes=True)
        add("g", fn, [], [out], 0.14 + 2 * CYC * size(out))

    def asel(out, in_, pat, op, fill, base, ch):
        add("g", lambda: g.affine_select(ap(out), ap(in_), pat, op, fill, base, ch), [in_], [out], 0.18 + 2 * CYC * size(out))

    def quant(q, p, a, b, in_):
        add("v", lambda: g.vector.quantize_mx(ap(R(q, a, b)), ap(R(p, a, b)), ap(in_)), [in_], [R(q, a, b), R(p, a, b)],
            0.02 + 0.00025 * size(in_))

    def mm(bank, wq, wp, wa, xq, xp, a, b):
        out = R("ps", 512 * bank, 512 * bank + b - a)
        rs = [R(wq, wa, wa + 128), R(wp, wa, wa + 128), R(xq, a, b), R(xp, a, b)]
        add("p", lambda: g.tensor.matmul_mx(ap(out), ap(rs[0]), ap(rs[1]), ap(rs[2]), ap(rs[3]), True, True), rs, [out],
            0.0008 * (b - a + 16))

    def dma(e, out, in_, rd, wr, lat, acc=False):
        def fn():
            if acc:
                return g.dma_start(out(), in_(), accum_op=A.add)
            return eng[e].dma_start(out(), in_())
        add(e, fn, rd, wr, 0.9 if e == "g" else 0.1, "d", lat)

    def accumulate(out, in_):
        dma("g", lambda: ap(out), lambda: ap(in_), [in_, out], [out], 2.5, True)

    def u8(r):
        return ap(r).bitcast(dt.uint8) if SCRATCH[r[0]][2] == Q else ap(r)

    def mask(es):
        return sum(1 << e for e in es)

    def send(peer, items, part):
        rid, pid = topo.addr(peer)[:2]
        es = part(topo.engines(core, peer))
        def fn():
            if len(items) == 1:
                return g.remote_dma(u8(items[0][1]), u8(items[0][0]), T.sem[items[0][2]], T.sem.sent, pid, rid, mask(es[0]))
            return g.remote_dma_fused([RemoteDMATransfer(dst_ids=[DstId(rid=rid, pnc=pid)], dma_engine_mask=mask(es[k]),
                                                         remote_sem=T.sem[x[2]], src=u8(x[0]), dst=u8(x[1]))
                                       for k, x in enumerate(items)], local_sem=T.sem.sent)
        k = add("g", fn, [x[0] for x in items], [], 0.7, "r", cnt=sum(len(e) for e in es))
        for x, e in zip(items, es):
            add("a", None, [], [x[1]], 0.0, "a", x[3], k, x[2], len(e))

    free = {"sm": 0, "of": 0, "li": 0}

    def new(buf, n):
        a = free[buf]
        free[buf] = a + n + (n & 1)
        return R(buf, a, a + n)

    def sub(r, a, b, s=1):
        return R(r[0], r[1] + a * r[3], min(r[2], r[1] + b * r[3]), r[3] * s)

    def bank(k, a, b):
        return R("ps", 512 * k + a, 512 * k + b)

    peer = [T.cores[rank ^ s] for s in STEP]
    low = [rank < (rank ^ s) for s in STEP]
    first = [0 if l else SL for l in low]
    pfirst = [SL - f for f in first]
    allE = lambda es: [es]
    three = lambda es: [es[len(es) // 2:], es[:len(es) // 4], es[len(es) // 4:len(es) // 2]]

    dma("y", lambda: T.lraw[:, 0:20], lambda: T.ri[:], [], [R("lraw", 0, 20)], 1.9)
    dma("s", lambda: T.lraw[:, 40:41], lambda: T.ro[:], [], [R("lraw", 40, 41)], 1.9)
    dma("y", lambda: T.lraw[:, 20:40], lambda: T.le[:], [], [R("lraw", 20, 40)], 1.9)
    dma("s", lambda: T.xt[:, 0:1280], lambda: T.x[:], [], [R("xt", 0, 1280)], 3.0)
    dma("y", lambda: T.ut[:], lambda: T.u[:], [], [R("ut", 0, 512)], 3.3)
    dma("y", lambda: T.wq[:].bitcast(dt.uint8), lambda: T.wc[:], [R("ut", 0, 512)], [R("wq", 0, 512)], 3.0)
    dma("y", lambda: T.wp[:], lambda: T.ws[:], [R("ut", 0, 512)], [R("wp", 0, 512)], 3.0)
    dma("y", lambda: T.vt[:], lambda: T.v[:], [R("ut", 0, 512)], [R("vt", 0, 512)], 3.0)

    pi, pj = new("li", 2), new("li", 2)
    iota(pi, [[16, 2]], 0, 1)
    mcol, h16, nh16 = new("sm", 1), new("sm", 1), new("sm", 1)
    ti = new("li", 2)
    ts(sub(ti, 0, 1), sub(pi, 0, 1), 16, None, A.bitwise_and)
    cp(h16, sub(ti, 0, 1))
    ts(sub(ti, 1, 2), sub(pi, 0, 1), 15, None, A.bitwise_and)
    cp(mcol, sub(ti, 1, 2))
    ts(pj, pi, 31, None, A.bitwise_and)
    oroot = new("of", 2)
    ts(oroot, pj, 672.0, None, A.add)
    lin(nh16, h16, -1.0, 0.0)
    mset(R("tin", 0, 704), 0.0)
    zz = new("sm", 2)
    mset(zz, 0.0)
    ts(R("tin", 640, 672, 16), zz, h16, 640.0, A.add, A.add)
    mset(R("half", 0, 516), 0.5)
    asel(R("ec", 0, 516), R("half", 0, 516), [[-1, 516]], A.is_equal, 0.0, 3, 4)
    for b in range(4):
        quant("eq", "ep", 128 * b, 128 * b + 128, R("ec", 3 - b, 515 - b))
    iota(R("zf", 0, 512), [[0, 512]], 0, 0)
    iota(R("lt", 0, 512), [[0, 512]], 0, 0)
    iota(R("snd", 0, 96), [[0, 96]], 0, 0)
    mset(R("xt", 1280, 1344), 0.0)
    mset(R("dw", 1104, 4 * DWS, DWS), 0.0)
    mset(R("cw", 20, 96, 32), 0.0)
    mset(R("ones", 0, 252), 1.0)
    iota(R("io16", 0, 160), [[0, 10], [1, 16]], 0, 0)
    ts(R("m16", 0, 160), R("io16", 0, 160), mcol, None, A.is_equal)
    asel(R("k16", 0, 160), R("ones", 0, 160), [[0, 10], [1, 16]], A.is_gt, 0.0, 0, 0)
    qi = new("li", 28)
    iota(qi, [[16, 28]], 0, 0)
    cp(R("uo", 0, 8), sub(qi, 0, 8))
    q = new("sm", 28)
    ts(q, qi, mcol, None, A.add)
    ne, qe = new("sm", 10), new("sm", 10)
    iota(ne, [[-2048, 10]], 0, 0)
    tt(qe, sub(q, 0, 10), ne, A.add)
    q7, f7, i7, t7, j7, mn, mx = new("sm", 7), new("sm", 7), new("li", 7), new("sm", 7), new("sm", 7), new("sm", 7), new("sm", 7)
    lin(q7, sub(q, 0, 7), 1.0, -12.0, AF.Relu)
    lin(f7, q7, 0.1, -0.45)
    cp(i7, f7)
    ts(t7, i7, -10.0, None, A.mult)
    tt(j7, t7, q7, A.add)
    tt(mn, j7, i7, A.min)
    tt(mx, j7, i7, A.max)
    orho, oj, omn, omx, otr = new("of", 7), new("of", 7), new("of", 7), new("of", 7), new("of", 7)
    cp(orho, i7); cp(oj, j7); cp(omn, mn); cp(omx, mx)
    j10, j11 = new("sm", 7), new("sm", 7)
    lin(j10, j7, 10.0, 0.0)
    tt(j11, j10, i7, A.add)
    ts(otr, j11, 2.0, None, A.mult)
    f15, i15, t15, e15 = new("sm", 15), new("li", 15), new("sm", 15), new("sm", 15)
    lin(f15, sub(q, 0, 15), 1.0 / 21, -10.0 / 21)
    cp(i15, f15)
    ts(t15, i15, -21.0, None, A.mult)
    tt(e15, t15, sub(q, 0, 15), A.add)
    oseg = new("of", 15)
    cp(oseg, e15)
    for t in range(3):
        iota(R("thr", 252 * t, 252 * t + 252), [[1, 12], [0, 21]], 0, 0)
    mset(R("thr", 20, 756, 252), 1000.0)
    asel(R("k21", 0, 252), R("ones", 0, 252), [[0, 12], [1, 21]], A.is_gt, 0.0, 0, 0)
    asel(R("sig", 1, 201), R("ones", 0, 200), [[-1, 10], [1, 10], [0, 2]], A.is_ge, -1.0, 0, 0)
    asel(R("sig", 201, 401), R("ones", 0, 200), [[1, 10], [-1, 10], [0, 2]], A.is_gt, -1.0, 0, 0)
    mset(R("sig", 0, 400, 20), 0.0)
    yi, oy = new("li", 4), new("of", 4)
    iota(yi, [[16, 2], [0, 2]], 0, 0)
    ts(oy, yi, mcol, None, A.add)
    ts(R("sw", 0, 32), R("ones", 0, 32), h16, 639.0, A.add, A.add)

    t41, pv = new("li", 41), new("sm", 41)
    ts(t41, R("lraw", 0, 41), 496, None, A.bitwise_and)
    tt(pv, t41, R("lraw", 0, 41), A.add)
    for o in (0, 16):
        ts(R("tin", o, 640, 32), sub(pv, 0, 20), h16, None, A.add)
    ts(R("tin", 672, 704, 16), zz, sub(pv, 40, 41), h16, A.add, A.add)
    WL, WR, W12 = R("win", 0, 704), R("win", 704, 1408), R("win", 704, 2080)
    tr(WR, R("tin", 0, 704))
    lin(R("sw", 0, 20), sub(pv, 0, 20), 1.0, h16)
    tr(R("sw", 32, 64), R("sw", 0, 32))
    gat("s", R("sw", 64, 128), R("sw", 32, 64), oy)
    tr(R("sw", 128, 192), R("sw", 64, 128))
    o2 = new("of", 42)
    cp(sub(o2, 0, 42, 2), R("sw", 128, 149))
    cp(sub(o2, 1, 42, 2), R("sw", 160, 181))
    gat("s", R("win", 1408, 1760), WR, sub(o2, 0, 22))
    gat("v", R("win", 1760, 1920), WR, sub(o2, 22, 32))
    gat("v", R("win", 1920, 2080), WR, sub(o2, 32, 42))
    for o in (0, 16):
        lin(R("tin", o, 640, 32), sub(pv, 20, 40), 1.0, h16)
    for k in range(6):
        tr(R("win", 128 * k, min(128 * k + 128, 704)), R("tin", 128 * k, min(128 * k + 128, 704)))
    quant("xq", "xp", 0, 160, R("xt", 0, 640))
    quant("xq", "xp", 160, 336, R("xt", 640, 1344))
    oc0 = new("of", 6)

    def step(e, a, n, w, o):
        gat(e, R("gg", a, a + n), w, o)
        if a == 32 * OPT["xat"]:
            ops[-1]["rd"].append(R("xp", 0, 336))
        if a == 32 * OPT["eat"]:
            ops[-1]["rd"].append(R("ep", 0, 512))
        tr(R("tt", a, a + n), R("gg", a, a + n))

    def both(o, a, n):
        cp(sub(o, 0, n // 16), R("tt", a, a + n, 16))
        ts(sub(o, n // 16, n // 8), R("tt", a, a + n, 16), 704.0, None, A.add)
        return o

    step("v", 0, 32, WR, oroot)
    cp(sub(oc0, 0, 2), R("tt", 0, 32, 16))
    step("v", 32, 32, WR, sub(oc0, 0, 2))
    for i in (1, 3, 5, 7):
        step("v", 32 * i + 32, 64, W12, both(sub(oc0, 2, 6) if i == 1 else new("of", 4), 32 * i, 32))
    step("s", 320, 64, WL, sub(oc0, 0, 4))
    for s in (0, 2, 4, 6):
        step("s", 384 + 64 * s, 128, W12, both(new("of", 8), 320 + 64 * s, 64))

    def places(pos, out):
        n = size(pos)
        ki, t = new("li", n), new("sm", n)
        ts(ki, pos, nh16, 1.0 / 32, A.add, A.mult)
        ts(t, ki, -16.0, nh16, A.mult, A.add)
        tt(out, t, pos, A.add)

    CA = new("sm", 36)
    CR = [sub(CA, 12 * t, 12 * t + 12) for t in range(3)]
    mset(sub(CA, 10, 36, 12), float(C))

    send(peer[0], [(R("xq", 0, 320), R("pxq", 0, 320), "ax", 2.8)], allE)
    send(peer[0], [(R("xp", 0, 320), R("pxp", 0, 320), "axs", 2.8)], allE)
    for b in range(4):
        act(R("xw", XX + 336 * b, XX + 336 * b + 336), R("xt", b, 1344, 4), AF.Copy, 0.5)
    quant("uq", "up", 0, 128, R("ut", 0, 512))
    add("v", lambda: g.vector.tensor_copy(T.u2q[:, 0:128].bitcast(dt.uint32), T.uq[:, 0:128].bitcast(dt.uint32).indirect(T.uo[:, 0:8])),
        [R("uq", 0, 128), R("uo", 0, 8)], [R("u2q", 0, 128)], cost(128, True))
    act(R("u2p", 0, 128), R("up", 0, 128), AF.Copy, 1.0, None, R("uo", 0, 8))

    def decode(qn, pn, n, at, b0):
        for b in range(4):
            mm(b0 or b, "eq", "ep", 128 * b, qn, pn, 0, n)
            act(R("dw", DWS * b + at, DWS * b + at + n), bank(b0 or b, 0, n))

    decode("xq", "xp", 336, 608, 0)

    def xwin(b):
        return R("xw", XX + 336 * b, XX + 336 * b + 336)

    for (a, z, es) in ((0, OPT["cut"], "ssss"), (OPT["cut"], SL, "vsvs")):
        o = new("of", z - a)
        places(R("tt", 32 * a, 32 * z, 32), sub(CR[0], a, z))
        cp(o, sub(CR[0], a, z))
        for b in range(4):
            gat(es[b], R("b0", 64 * a + b, 64 * z, 4), xwin(b), o, 2.0)
    quant("b0q", "b0p", 0, 160, R("b0", 0, 640))
    mm(4, "u2q", "u2p", 0, "b0q", "b0p", 0, 160)

    def diag(bk, n, at):
        tt(R("sc1", at, at + n), bank(bk, 0, n), R("m16", 0, n), A.mult)
        scan(R("sc2", at, at + n), R("k16", 0, n), R("sc1", at, at + n), A.mult, A.add)
        return R("sc2", at + 15, at + n, 16)

    KO = [R("ko", 16 * t, 16 * t + 10) for t in range(3)]
    SK = [R("snd", 32 * t, 32 * t + 10) for t in range(3)]
    SB = [R("snd", 32 * t + 22, 32 * t + 32) for t in range(3)]
    MS = ["msg0", "msg1", "msg2"]
    cap, ncap, nl, e4, kn = [], [], [], [], []
    ZC = [640, 928, 816]
    WIN = [(288, 944), (0, 944), (288, 1105)]
    OWN = [(320, 0, 0), (608, 144, 1), (320, 656, 2)]
    PAR = [(0, 0, 0), (None, 272, 1), (0, 784, 2)]

    def tables(t):
        c = sub(CR[t], 0, 10)
        for l in (cap, ncap, nl, e4, kn):
            l.append(new("sm", 10))
        lin(cap[t], c, -BIG, 319.5 * BIG)
        lin(ncap[t], c, BIG if low[t] else -BIG, (-319.5 if low[t] else 319.5) * BIG)
        late = OWN[t][2]
        ce = new("sm", 10)
        tt(ce, c, ne, A.add)
        for (dst, k, (cx, cl, _)) in ((SB[t], 20.0 - pfirst[t], PAR[t]), (R(MS[t], 32, 42), 10.0 - first[t], OWN[t])):
            if cx is None:
                lin(sub(dst, late, 10), sub(qe, late, 10), UNIT, k - 16 * UNIT)
            else:
                lin(sub(dst, late, 10), sub(ce, late, 10), UNIT, k + cx * UNIT)
            if late:
                lin(sub(dst, 0, late), sub(qe, 0, late), UNIT, k + cl * UNIT)
        lin(e4[t], c, 4.0, -4.0 * (C - 1), AF.Relu)
        iota(kn[t], [[-1, 10]], -1 - first[t], 0)
        lin(nl[t], sub(CR[t], 1, 11), -16384.0, 16384.0 * C)

    def keys(t, s, a, b):
        tt(sub(SK[t], a, b), s, sub(ncap[t], a, b), A.max if low[t] else A.min)
        tt(sub(KO[t], a, b), s, sub(cap[t], a, b), A.min)

    def note(t):
        return (R("snd", 32 * t, 32 * t + 32), R(MS[t], 0, 32), "ak%d" % t, 2.0)

    tables(0)
    keys(0, diag(4, 160, 0), 0, 10)
    send(peer[0], [note(0)], allE)
    decode("pxq", "pxp", 320, 288, 0)

    c12 = new("sm", 18)
    places(R("tt", 320, 896, 32), c12)
    ob1, ob2 = new("of", 9), new("of", 8)
    cp(ob1, sub(c12, 0, 18, 2))
    cp(ob2, sub(c12, 1, 17, 2))
    act(sub(CR[1], 0, 1), sub(CR[0], 0, 1)); act(sub(CR[1], 1, 10), sub(c12, 0, 18, 2))
    act(sub(CR[2], 0, 2), sub(CR[0], 0, 2)); act(sub(CR[2], 2, 10), sub(c12, 1, 17, 2))
    for b in range(4):
        gat("s", R("be", b, 576, 4), xwin(b), ob1, 2.0)
    for b in range(4):
        gat("s", R("be", 576 + b, 1088, 4), xwin(b), ob2, 2.0)
    quant("beq", "bep", 0, 144, R("be", 0, 576))
    quant("beq", "bep", 144, 272, R("be", 576, 1088))
    send(peer[1], [(R("beq", 0, 144), R("pbq", 0, 144), "ab", 2.8)], allE)
    send(peer[1], [(R("bep", 0, 144), R("pbp", 0, 144), "abs_", 2.8)], allE)
    mm(5, "u2q", "u2p", 0, "beq", "bep", 0, 144)
    tables(1); tables(2)
    keys(1, diag(5, 144, 160), 1, 10)
    mm(5, "u2q", "u2p", 0, "beq", "bep", 144, 272)
    keys(2, diag(5, 128, 304), 2, 10)

    def last_lists():
        iota(R("lab", 0, 160), [[1, 160]], XH2, 0)
        iota(R("lab", 160, 288), [[4, 128]], XH0 + 128, 0)
        iota(R("lab", 288, 432), [[4, 144]], XH1 + 64, 0)
        pa, pb, dm = new("sm", 27), new("sm", 27), new("sm", 27)
        lin(dm, sub(q, 0, 27), 1.0, 672.0)
        act(sub(pa, 0, 2), R("tt", 0, 64, 32))
        act(sub(pa, 2, 10), R("tt", 352, 864, 64))
        act(sub(pa, 10, 18), R("tt", 64, 320, 32))
        act(sub(pa, 18, 27), R("tt", 320, 896, 64))
        lin(pb, pa, 2000.0, -639.0 * 2000.0)
        tt(pb, pb, dm, A.min)
        tt(pb, pb, pa, A.max)
        osc = new("of", 27)
        cp(osc, pb)
        iota(R("ws_", 0, 640), [[0, 640]], 0, 0)
        for a in range(0, 27, 6):
            o = sub(osc, a, min(a + 6, 27))
            s = R("lab", 16 * a, 16 * min(a + 6, 27))
            add("v", lambda o=o, s=s: g.vector.tensor_copy(ind(R("ws_", 0, 1104), o), ap(s)), [o, s], [R("ws_", 0, 1104)],
                CYC * (60 + 3.5 * size(s)))
        for k in range(4):
            tr(R("wt", 160 * k, 160 * k + 160), R("ws_", 160 * k, 160 * k + 160))
        lb, f0, xi, x2, ix = new("sm", 20), new("sm", 20), new("sm", 20), new("sm", 20), new("sm", 20)
        s1, s2, st = new("sm", 20), new("sm", 20), new("sm", 20)
        tt(lb, R("wt", 0, 640, 32), R("wt", 16, 640, 32), A.add)
        lin(xi, sub(q, 0, 20), 1.0, float(XX))
        lin(f0, lb, -1.0, 1.0, AF.Relu)
        tt(x2, xi, f0, A.mult)
        tt(ix, x2, lb, A.add)
        lin(s1, f0, 335.0, 1.0)
        ts(s2, lb, float(XH2), 159.0, A.is_ge, A.mult)
        tt(st, s1, s2, A.add)
        out = []
        for b in range(4):
            out.append(new("of", 20))
            cp(out[b], ix)
            if b < 3:
                nx = new("sm", 20)
                tt(nx, ix, st, A.add)
                ix = nx
        f1, f2, d = new("sm", 20), new("sm", 20), new("sm", 20)
        lin(f1, lb, 1.0, -(XH2 + 23.5), AF.Abs)
        ts(f2, f1, 8.0, None, A.is_lt)
        tt(f2, f2, f0, A.add)
        tt(d, R("lraw", 20, 40), R("lraw", 0, 20), A.subtract)
        tt(d, d, f2, A.mult)
        iota(R("oi", 0, 64), [[0, 64]], 0, 0)
        tt(R("oi", 0, 20), d, R("lraw", 0, 20), A.add)
        tt(R("oi", 32, 52), R("lraw", 20, 40), d, A.subtract)
        tr(R("ot", 0, 64), R("oi", 0, 64))
        for k in range(4):
            dma("y", lambda k=k: T.od[k:16:4, :], lambda k=k: T.ot[:, 32 * (k % 2) + 16 * (k // 2):32 * (k % 2) + 16 * (k // 2) + 16],
                [R("ot", 0, 64)], [R("od", k, k + 1)], 2.2)
        dma("y", lambda: T.ol[:], lambda: T.od[:, 0:C], [R("od", 0, 4)], [], 2.2)
        return out

    def order(t):
        y0, c0, s0 = 336 * t, 432 * t, 400 * t
        PK = R(MS[t], 0, 10)
        Y = [R("yy", y0 + 112 * k, y0 + 112 * k + 112) for k in range(3)]
        gat("s", Y[0], KO[t], omx)
        gat("s", Y[1], KO[t], orho)
        tt(R("cc", c0 + 201, c0 + 424, 2), KO[t], Y[0], A.is_ge, omn)
        gat("s", Y[2], PK, omx)
        tt(R("cc", c0 + 200, c0 + 424, 2), PK, Y[1], A.is_gt if low[t] else A.is_ge, oj)
        gat("s", R("cc", c0, c0 + 224, 2), R("cc", c0 + 224, c0 + 424), otr)
        tt(R("cc", c0 + 1, c0 + 224, 2), PK, Y[2], A.is_ge, omn)
        scan(R("thr", 252 * t + 41, 252 * t + 232, 21), kn[t], e4[t], A.add, A.subtract, 1000.0)
        scan(R("cs", s0, s0 + 400), R("sig", 0, 400), R("cc", c0 + 24, c0 + 424), A.mult, A.add)
        tt(R("cw", 32 * t, 32 * t + 20), R(MS[t], 22, 42), R("cs", s0 + 19, s0 + 400, 20), A.subtract)

    DF = new("sm", 36)
    mset(sub(DF, 10, 36, 12), 4.0)

    def sums(t, at, n):
        tt(R("mm", at, at + n), R("cw", 32 * t, 32 * t + 21), R("thr", 252 * t, 252 * t + n), A.max, sub(oseg, 0, n // 16))
        scan(R("ms", at, at + n), R("k21", 0, n), R("mm", at, at + n), A.mult, A.add)

    def dwin(t, b):
        return R("dw", DWS * b + WIN[t][0], DWS * b + WIN[t][1])

    def fast(t):
        at = 720 + 64 * t
        sums(t, at, 64)
        G = [R("ms", at + 20 + 21 * i, at + 21 + 21 * i) for i in range(3)]
        oa, on, d0, d1 = new("of", 1), new("of", 1), new("sm", 1), new("sm", 1)
        ts(oa, G[0], G[1], 2048.0, A.subtract, A.mult)
        ts(d0, G[0], G[1], 2048.0, A.subtract, A.mult)
        ts(d1, G[1], G[2], 2048.0, A.subtract, A.mult)
        ts(on, d0, sub(nl[t], 0, 1), d1, A.add, A.min)
        e0 = 128 * t
        for b in range(4):
            gat("s", R("ef", e0 + b, e0 + 64, 4), dwin(t, b), oa)
            tt(R("zf", b, 64, 4), dwin(t, b), R("ef", e0 + b, e0 + 64, 4), A.add, on)
        act(R("ef", e0 + 64, e0 + 128), R("ef", e0, e0 + 64), AF.Copy, 2.0)
        quant("zfq", "zfp", 128 * t, 128 * t + 128, R("zf", 0, 512))
        for b in range(4):
            mm(b, "wq", "wp", 128 * b, "zfq", "zfp", 128 * t, 128 * t + 128)
            act(R("tf", 64 * t + b, 64 * t + 64, 4), bank(b, 0, 16), AF.Relu, 0.03125)
        tt(R("lt", 0, 64), R("tf", 64 * t, 64 * t + 64), R("ef", e0 + 64, e0 + 128), A.add)
        qn, pn = ("l1q", "l1p") if t == 0 else ("l2q", "l2p")
        quant(qn, pn, 0, 128, R("lt", 0, 512))
        mm(4, "u2q", "u2p", 0, qn, pn, 0, 128)
        if t == 0:
            tt(R("sc1", 432, 448), bank(4, 0, 16), R("m16", 0, 16), A.mult)
            red(sub(SK[1], 0, 1), R("sc1", 432, 448))
            red(sub(KO[1], 0, 1), R("sc1", 432, 448))
        else:
            keys(2, diag(4, 32, 448), 0, 2)
        send(peer[t + 1], [note(t + 1), (R(qn, 0, 32), R(qn, 128, 160), "al%d" % (t + 1), 2.5),
                           (R(pn, 0, 128), R(pn, 128, 256), "as%d" % (t + 1), 2.5)], three)

    def full(t):
        at = 240 * t
        sums(t, at, 240)
        df = sub(DF, 12 * t, 12 * t + 11)
        tt(sub(df, 0, 10), R("ms", at + 20, at + 210, 21), R("ms", at + 41, at + 231, 21), A.subtract)
        oa, on, nf = new("of", 10), new("of", 10), new("sm", 10)
        ts(oa, sub(df, 0, 10), 2048.0, float(ZC[t]), A.mult, A.min)
        tt(nf, sub(df, 0, 10), nl[t], A.add)
        tt(nf, nf, sub(df, 1, 11), A.min)
        ts(on, nf, 2048.0, float(ZC[t]), A.mult, A.min)
        e0 = 640 * t
        E = [R("eh", e0 + b, e0 + 640, 4) if t < 2 else R("eh", e0 + 160 * b, e0 + 160 * b + 160) for b in range(4)]
        for b in range(4):
            gat(OPT["e2"][b] if t == 2 else "s", E[b], dwin(t, b), oa)
            if t < 2 and OPT["z"][t] == "d":
                gat("s", R("zt", e0 + b, e0 + 640, 4), dwin(t, b), on)
            else:
                tt(R("zt", e0 + b, e0 + 640, 4), dwin(t, b), E[b], A.add, on)
        if t < 2 and OPT["z"][t] == "d":
            accumulate(R("zt", e0, e0 + 640), R("eh", e0, e0 + 640))
        quant("zq", "zp", 160 * t, 160 * t + 160, R("zt", e0, e0 + 640))
        h0 = [XH0, XH1, XH2][t]
        if t == 0:
            e1, o1 = new("sm", 1), new("of", 1)
            lin(e1, sub(CR[0], 1, 2), 16.0, 0.0)
            ts(o1, e1, -16.0 * (C - 1), mcol, A.add, A.max)
            mset(R("t2", 16, 128, 32), 0.0)
            act(R("ef", 256, 320), R("eh", 64, 128), AF.Copy, 2.0)
        for b in range(4):
            bk = b if t == 2 else 6 + (b & 1)
            mm(bk, "wq", "wp", 128 * b, "zq", "zp", 160 * t, 160 * t + 160)
            if t == 0:
                w = R("t2", 32 * b, 32 * b + 17)
                act(sub(w, 0, 16), bank(bk, 16, 32), AF.Relu, 0.03125)
                tt(R("lt", 64 + b, 128, 4), w, R("ef", 256 + b, 320, 4), A.add, o1)
            if t < 2:
                act(R("xw", h0 + b, h0 + 640, 4), bank(bk, 0, 160), AF.Relu, 0.015625)
            else:
                act(R("t2", 160 * b, 160 * b + 160), bank(b, 0, 160), AF.Relu, 0.015625)
                tt(R("xw", h0 + 160 * b, h0 + 160 * b + 160), R("t2", 160 * b, 160 * b + 160), E[b], A.add)
        if t < 2:
            accumulate(R("xw", h0, h0 + 640), R("eh", e0, e0 + 640))

    order(0)
    fast(0)
    decode("pbq", "pbp", 144, 0, 5)
    full(0)
    order(1)
    decode("l1q", "l1p", 144, 144, 0)
    fast(1)
    full(1)
    olast = last_lists()
    quant("vq", "vp", 0, 128, R("vt", 0, 512))
    order(2)
    decode("l2q", "l2p", 160, 944, 0)
    full(2)
    for b in range(4):
        for h in range(2):
            gat(OPT["last"][2 * b + h], R("xo", 640 * h + b, 640 * h + 640, 4), R("xw", 0, XH2 + 160 * b + 160),
                sub(olast[b], 10 * h, 10 * h + 10), 2.0)
    for h in range(2):
        a, z = 160 * h, 160 * h + 160
        quant("oq", "op", a, z, R("xo", 4 * a, 4 * z))
        mm(4 + h, "vq", "vp", 0, "oq", "op", a, z)
        act(R("ys", a, z), bank(4 + h, 0, 160))
    dma("s", lambda: T.y[:], lambda: T.ys[:], [R("ys", 0, C)], [], 2.1)
    dma("y", lambda: T.oc[:], lambda: T.oq[:].bitcast(dt.uint8), [R("oq", 0, C)], [], 2.1)
    for k in range(4):
        dma(OPT["osc"][k], lambda k=k: T.osc[4 * k:4 * k + 4, 0:C], lambda k=k: T.op[32 * k:32 * k + 4, 0:C], [R("op", 0, C)], [], 1.9)
    return ops, eng


def links(ops):
    seen, pred = {}, []
    for k, o in enumerate(ops):
        ps = set()
        if o["after"] is not None:
            ps.add(o["after"])
        acc = [(r[0], bits(r), r[0] == "ps") for r in o["rd"]] + [(r[0], bits(r), True) for r in o["wr"]]
        for name, m, w in acc:
            for j, mj, wj in seen.get(name, []):
                if j != k and (w or wj) and m & mj:
                    ps.add(j)
        for name, m, w in acc:
            seen.setdefault(name, []).append((k, m, w))
        pred.append(sorted(ps))
    return pred


def schedule(ops, pred):
    n = len(ops)
    E, c, l = [o["e"] for o in ops], [o["cost"] for o in ops], [o["lat"] for o in ops]
    pf, pb = [[] for o in ops], [[] for o in ops]
    for k in range(n):
        for j in pred[k]:
            d = l[j] + (0.0 if E[k] == "a" else OPT["near"] if E[j] == E[k] else OPT["far"])
            pf[k].append((j, d))
            pb[j].append((k, d))
    cases = []
    for (near, far, di, ra, rl, cf) in CASES:
        cc = [di if o["kind"] == "d" and o["e"] != "g" else ra if o["kind"] == "r" else o["cost"] * cf if o["kind"] == "c" else o["cost"] for o in ops]
        ll = [o["lat"] + (rl - 0.4 if o["kind"] == "a" else 0.0) for o in ops]
        cases.append((cc, ll, [[(j, 0.0 if E[k] == "a" else near if E[j] == E[k] else far) for j in pred[k]] for k in range(n)]))

    def replay(seq):
        out = []
        for cc, ll, pp in cases:
            fr, dn = {e: 0.0 for e in ENG}, [0.0] * n
            for k in seq:
                t = fr.get(E[k], 0.0)
                for j, d in pp[k]:
                    if dn[j] + d > t:
                        t = dn[j] + d
                t += cc[k]
                if E[k] != "a":
                    fr[E[k]] = t
                dn[k] = t + ll[k]
            out.append(max(dn))
        return out

    def place(key, P, t0):
        busy, end = {e: ([], []) for e in ENG}, [None] * n
        def put(k):
            t = t0[k]
            for j, d in P[k]:
                if end[j] is None:
                    put(j)
                if end[j] + d > t:
                    t = end[j] + d
            if E[k] != "a":
                S, Z = busy[E[k]]
                i = len(Z)
                while i and Z[i - 1] > t:
                    i -= 1
                while i < len(S) and t + c[k] > S[i] + 1e-9:
                    t = Z[i]
                    i += 1
                S.insert(i, t)
                Z.insert(i, t + c[k])
            end[k] = t + c[k]
        for k in sorted(range(n), key=lambda k: -key[k]):
            if end[k] is None:
                put(k)
        return end

    zero, cur, best, now, rnd = [0.0] * n, [0.0] * n, None, None, OPT["seed"]
    for k in range(n - 1, -1, -1):
        cur[k] = c[k] + 1e-6 + max([cur[j] + d for j, d in pb[k]] + [l[k]])
    for it in range(OPT["iters"]):
        key = cur[:]
        rnd = (rnd * 1103515245 + 12345) % 2147483648
        kind = (rnd >> 8) % 8
        for r in range(1 + (rnd >> 12) % 3 if it else 0):
            rnd = (rnd * 1103515245 + 12345) % 2147483648
            k = (rnd >> 8) % n
            rnd = (rnd * 1103515245 + 12345) % 2147483648
            u = rnd / 2147483648.0 - 0.5
            key[k] += u * abs(u) * (24.0 if kind < 4 else 3.0)
        e = place(key, pf, zero)
        if kind == 7:
            e = place(place([e[k] + l[k] for k in range(n)], pb, l), pf, zero)
        seq = sorted(range(n), key=lambda k: (e[k] - c[k], k))
        times = replay(seq)
        m = sum(times) / len(times)
        w = m + OPT["mean"] * sum(e) / n
        rnd = (rnd * 1103515245 + 12345) % 2147483648
        if now is None or w <= now + OPT["heat"] * (1.0 - it / OPT["iters"]) * (rnd / 2147483648.0) ** 4:
            now, cur = w, [c[k] - e[k] for k in range(n)]
        if best is None or m < best[0]:
            best = (m, seq, [e[k] + l[k] for k in range(n)], times)
    return best[1], best[3], best[2]


def rank_program(g, core, T, topo):
    rank = T.rank_of(core)
    if rank is None:
        return
    ops, eng = build(g, core, T, topo, rank)
    pred = links(ops)
    if "order" not in KEPT:
        KEPT["order"] = schedule(ops, pred)
    seq, times, done = KEPT["order"]
    count = {e: 0 for e in ENG}
    know = {e: {} for e in ENG}
    mark, clock, total, nd = {}, {}, {}, [0]
    for k in seq:
        o = ops[k]
        if o["kind"] == "a":
            mark[k], clock[k] = (o["sem"], o["cnt"]), {o["sem"]: o["cnt"]}
            total[o["sem"]] = o["cnt"]
            continue
        e = o["e"]
        need = {}
        for j in pred[k]:
            s, n = mark[j]
            if n > need.get(s, (0, 0))[0]:
                need[s] = (n, j)
        for s, (n, j) in sorted(need.items(), key=lambda x: -done[x[1][1]]):
            if know[e].get(s, 0) < n:
                eng[e].wait_ge(T.sem[s], n)
                for s2, n2 in clock[j].items():
                    know[e][s2] = max(know[e].get(s2, 0), n2)
        ins = o["fn"]()
        if o["kind"] == "c":
            count[e] += 1
            mark[k] = ("e" + e, count[e])
            ins.then_inc(T.sem["e" + e], 1)
        elif o["kind"] == "d":
            mark[k] = ("d%d" % nd[0], 16)
            nd[0] += 1
            ins.then_inc(T.sem[mark[k][0]], 16)
        else:
            total["sent"] = total.get("sent", 0) + o["cnt"]
            continue
        total[mark[k][0]] = mark[k][1]
        clock[k] = dict(know[e])
        clock[k][mark[k][0]] = mark[k][1]
    for s, n in sorted(total.items()):
        if know["y"].get(s, 0) < n:
            g.sync.wait_ge(T.sem[s], n)
